import numpy as np
import ml_dtypes


def mxq(x, axis, fmt="e4m3"):
    dtype, down = {"e4m3": (ml_dtypes.float8_e4m3fn, 7), "e5m2": (ml_dtypes.float8_e5m2, 14)}[fmt]
    v = np.moveaxis(np.asarray(x, np.float32).astype(ml_dtypes.bfloat16).astype(np.float64), axis, -1)
    blocks = v.reshape(v.shape[:-1] + (-1, 32))
    amax = np.abs(blocks).max(-1, keepdims=True)
    byte = np.maximum(np.where(amax > 0, np.frexp(amax)[1] - 1 + 127, 0) - down, 1)
    scale = np.exp2(byte - 127.0)
    codes = (blocks / scale).astype(np.float32).astype(dtype).astype(np.float64)
    return np.moveaxis((codes * scale).reshape(v.shape), -1, axis)


WIDE = False


def mx_kscale(k):
    if not WIDE:
        return np.ones(k)
    levels = np.array([10, -10, 5, -5, 0])
    if k % 512:
        return np.exp2(np.random.permutation(np.resize(levels, k // 32))).repeat(32)
    a = np.empty((k // 512, 16))
    for p in range(k // 512):
        a[p, :8] = np.random.permutation(np.resize(levels, 8))
        for g in range(8):
            far = levels[np.abs(levels - a[p, g]) >= 10]
            a[p, g + 8] = far[np.random.randint(len(far))]
    return np.exp2(a.ravel()).repeat(32)


def f64(x):
    return np.asarray(x).astype(np.float64)


def striped(idx):
    return np.tile(idx.reshape(-1, 16).T, (8, 1)).astype(np.uint16)


def unstriped(offs):
    return offs[:16].T.reshape(-1).astype(np.int64)


E2M1 = np.array([0.0, 0.5, 1.0, 1.5, 2.0, 3.0, 4.0, 6.0, -0.0, -0.5, -1.0, -1.5, -2.0, -3.0, -4.0, -6.0])


def pack_weight(w, fmt):
    k, n = w.shape
    w = f64(np.asarray(w, np.float32).astype(ml_dtypes.bfloat16)).reshape(k // 32, 32, n)
    amax = np.abs(w).max(1)
    if fmt == "e4m3":
        byte = np.frexp(amax)[1] - 1 + 127 - 7
    else:
        mant, ex = np.frexp(amax / 6.0)
        byte = np.where(mant > 0.5, ex, ex - 1) + 127
    byte = np.clip(np.where(amax > 0, byte, 1), 1, 254)
    scaled = (w * np.exp2(127.0 - byte)[:, None, :]).reshape(k, n).astype(np.float32)
    by_word = np.ascontiguousarray(scaled.reshape(k // 512, 128, 4, n).transpose(0, 1, 3, 2))
    if fmt == "e4m3":
        words = by_word.astype(ml_dtypes.float8_e4m3fn).view(np.uint8)
    else:
        c = by_word.astype(ml_dtypes.float4_e2m1fn).view(np.uint8) & 0xF
        words = (c[..., 0::2] | (c[..., 1::2] << 4)).reshape(k // 512, 128, 2 * n)
    return np.ascontiguousarray(words), np.ascontiguousarray(byte.astype(np.uint8).reshape(k // 512, 16, n))


def unpack_weight(words, scales, fmt):
    g, _, n = scales.shape
    words = np.ascontiguousarray(words).reshape(g, 128, n, -1)
    if fmt == "e4m3":
        vals = words.view(ml_dtypes.float8_e4m3fn).astype(np.float64)
    else:
        nib = np.empty((g, 128, n, 4), np.uint8)
        nib[..., 0::2] = words & 0xF
        nib[..., 1::2] = words >> 4
        vals = E2M1[nib]
    vals = vals * np.repeat(np.exp2(scales.astype(np.float64) - 127.0), 8, axis=1)[..., None]
    return vals.transpose(0, 1, 3, 2).reshape(g * 512, n)


def gelu(v):
    return 0.5 * v * (1.0 + np.tanh(np.sqrt(2.0 / np.pi) * (v + 0.044715 * v**3)))


def often(T, S):
    return np.random.permutation(T)[(T * np.random.uniform(0, 1, S) ** 4).astype(np.int64)]


K, T, S, H, N = 1024, 4096, 1024, 1024, 384

def setup_inputs():
    n = np.random.standard_normal
    s = mx_kscale(K)[:, None]
    u = mx_kscale(H)[:, None]
    tab_words, tab_scales = pack_weight(n((K, T)) * s, "e4m3")
    tab2_words, tab2_scales = pack_weight(n((K, T)) * s, "e2m1")
    w8_words, w8_scales = pack_weight(n((K, H)) / np.sqrt(K) / s * u.T, "e4m3")
    return {
        "tab_words": tab_words, "tab_scales": tab_scales,
        "offs": striped(often(T, S)),
        "tab2_words": tab2_words, "tab2_scales": tab2_scales,
        "offs2": striped(often(T, S)),
        "w8_words": w8_words, "w8_scales": w8_scales,
        "dm": (0.5 * n(H) * u[:, 0]).astype(np.float32),
        "wv": (n((H, N)) / np.sqrt(H) / u).astype(np.float32),
        "bv": (0.5 * n(N)).astype(np.float32),
    }

def reference(tab_words, tab_scales, offs, tab2_words, tab2_scales, offs2, w8_words, w8_scales, dm, wv, bv):
    v = unpack_weight(tab_words, tab_scales, "e4m3")[:, unstriped(offs)]
    v2 = unpack_weight(tab2_words, tab2_scales, "e2m1")[:, unstriped(offs2)]
    w8 = unpack_weight(w8_words, w8_scales, "e4m3")
    a = w8.T @ v
    b = w8.T @ v2
    h = np.abs(a - b + f64(dm)[:, None])
    y = mxq(f64(wv), 0, "e4m3").T @ mxq(h, 0, "e4m3")
    return 1.0 / (1.0 + np.exp(-(y + f64(bv)[:, None])))

@@ -1,0 +1,234 @@
+from contextlib import ExitStack
+
+import concourse.mybir as mybir
+from concourse.masks import make_identity
+
+K, T, S, H, N = 1024, 4096, 1024, 1024, 384
+FLOPS = 2 * 2 * K * H * S + 2 * H * N * S
+
+F32 = mybir.dt.float32
+BF16 = mybir.dt.bfloat16
+I32 = mybir.dt.int32
+U32 = mybir.dt.uint32
+U16 = mybir.dt.uint16
+U8 = mybir.dt.uint8
+FP8X4 = mybir.dt.float8_e4m3fn_x4
+FP4X4 = mybir.dt.float4_e2m1fn_x4
+ACT = mybir.ActivationFunctionType
+ADD = mybir.AluOpType.add
+
+P = 128
+HALF = 512
+CHUNK = 128
+GROUPS = (512, 256, 128, 128)
+TAB_ROW = 8
+
+
+def tile_list_loop_closure_vetting_kernel(
+    tc, tab_words, tab_scales, offs, tab2_words, tab2_scales, offs2, w8_words, w8_scales, dm, wv, bv, out
+):
+    nc = tc.nc
+    with ExitStack() as ctx:
+        keep = ctx.enter_context(tc.tile_pool(name="keep", bufs=1))
+        ring = ctx.enter_context(tc.tile_pool(name="ring", bufs=4))
+        psum = ctx.enter_context(tc.psum_pool(name="psum", bufs=8))
+
+        def held(shape, dtype, name):
+            return keep.tile(shape, dtype, name=name, align_bytes=64)
+
+        list1 = held([P, S // 16], U16, "list1")
+        list2 = held([P, S // 16], U16, "list2")
+        tab = [held([P, T], I32, "tab%d" % a) for a in range(2)]
+        tab2 = [held([P, T // 2], I32, "tab2_%d" % a) for a in range(2)]
+        tab_sc = held([P, T // 4], I32, "tab_sc")
+        tab2_sc = held([P, T // 4], I32, "tab2_sc")
+        w8_raw = held([P, 2 * H], I32, "w8_raw")
+        w8 = held([P, 2 * H], I32, "w8")
+        w8_sc_raw = held([P, 2 * H // 4], I32, "w8_sc_raw")
+        w8_sc = held([P, 2 * H // 4], I32, "w8_sc")
+        rows = held([P, P], F32, "rows")
+        ident = held([P, P], F32, "ident")
+        cols = held([P, 16], F32, "cols")
+        warm = held([P, 1], F32, "warm")
+        shifted = [held([P, HALF // 4], I32, "shifted%d" % h) for h in range(2)]
+        wv_raw = [held([P, 4, N], F32, "wv_raw%d" % b) for b in range(2)]
+
+        make_identity(nc, ident[:])
+        nc.vector.memset(tab2_sc[:], 0)
+        nc.vector.memset(w8_sc_raw[:], 0)
+        nc.vector.memset(rows[:], 0.0)
+        nc.vector.memset(tab_sc[:], 0)
+        for h in range(2):
+            nc.vector.memset(shifted[h][:], 0)
+        nc.scalar.activation(warm[:], rows[:, 0:1], ACT.Sigmoid)
+
+        nc.sync.dma_start(list2[:], offs2)
+        nc.sync.dma_start(
+            w8_raw[:].rearrange("p (a c) -> p a c", a=2),
+            w8_words.rearrange("a p c i -> p a (c i)").bitcast(I32),
+        )
+        nc.sync.dma_start(tab2[0][:], tab2_words[0].bitcast(I32))
+        for q in range(4):
+            nc.gpsimd.dma_start(tab2_sc[32 * q : 32 * q + 8, :], tab2_scales[:, 4 * q : 4 * q + 4, :].bitcast(I32))
+        for q in range(4):
+            nc.scalar.dma_start(
+                w8_sc_raw[32 * q : 32 * q + 4, :].rearrange("r (a c) -> r a c", a=2),
+                w8_scales[:, 4 * q : 4 * q + 4, :].rearrange("a r c -> r a c").bitcast(I32),
+            )
+        nc.sync.dma_start(tab2[1][:], tab2_words[1].bitcast(I32))
+        for b in range(2):
+            nc.scalar.dma_start(
+                rows[4 * b : 4 * b + 4, :].rearrange("t (g i) -> t g i", i=8),
+                dm[512 * b : 512 * (b + 1)].rearrange("(g t i) -> t g i", t=4, i=8),
+            )
+        nc.scalar.dma_start(rows[8:11, :], bv.rearrange("(m p) -> m p", p=P))
+        nc.sync.dma_start(list1[:], offs)
+        for a in range(2):
+            nc.sync.dma_start(tab[a][:], tab_words[a].rearrange("p c i -> p (c i)").bitcast(I32))
+        for q in range(4):
+            nc.gpsimd.dma_start(
+                tab_sc[32 * q + TAB_ROW : 32 * q + TAB_ROW + 8, :], tab_scales[:, 4 * q : 4 * q + 4, :].bitcast(I32)
+            )
+        for b in range(2):
+            by_slot = wv[512 * b : 512 * (b + 1), :].rearrange("(g t i) n -> t g i n", t=4, i=8)
+            for t in range(4):
+                nc.sync.dma_start(wv_raw[b][:, t, :], by_slot[t])
+
+        turned = psum.tile([P, HALF], F32, name="bank")
+        nc.tensor.transpose(turned[:, 0:P], rows[:], ident[:])
+        nc.scalar.copy(cols[:], turned[:, 0:16])
+
+        nc.vector.tensor_copy(
+            w8[:].rearrange("p (u t g i) -> p u t g i", u=4, t=4, i=8),
+            w8_raw[:].rearrange("p (u g t i) -> p u t g i", u=4, t=4, i=8),
+        )
+        nc.vector.tensor_copy(
+            w8_sc[:].rearrange("p (u t g i) -> p u t g i", u=4, t=4, i=2),
+            w8_sc_raw[:].rearrange("p (u g t i) -> p u t g i", u=4, t=4, i=2),
+        )
+
+        def half_of(offsets, h):
+            return offsets[:, h * HALF // 16 : (h + 1) * HALF // 16]
+
+        def gather(window, offsets, h, dtype, name):
+            picked = held([P, HALF], dtype, name)
+            nc.vector.tensor_copy(picked[:], window[:].bitcast(dtype).indirect(half_of(offsets, h)))
+            return picked
+
+        def w8_operand(a, r):
+            c = slice(a * H + r * P, a * H + (r + 1) * P)
+            return w8[:, c].bitcast(FP8X4), w8_sc[:].bitcast(U8)[:, c]
+
+        neg_b = [[held([P, 4, HALF], F32, "neg_b%d%d" % (h, b)) for b in range(2)] for h in range(2)]
+        shift_queue = (nc.scalar, nc.gpsimd)
+        for h in range(2):
+            sc2 = gather(tab2_sc, list2, h, U8, "sc2_%d" % h)
+            shift_queue[h].dma_start(shifted[h][0:112, :], sc2[4:116, :].bitcast(I32))
+            v2 = [gather(tab2[a], list2, h, U16, "v2_%d%d" % (h, a)) for a in range(2)]
+            planes = (sc2[:], shifted[h][:].bitcast(U8))
+
+            def archive_pass(bank, a, r):
+                codes, scale = w8_operand(a, r)
+                nc.tensor.matmul_mx(
+                    out=bank[:], lhsT=codes, lhsT_scale=scale, rhs=v2[a][:].bitcast(FP4X4), rhs_scale=planes[a],
+                    start=(a == 0), stop=(a == 1),
+                )
+
+            ahead = 4 if h == 0 else 0
+            banks = [psum.tile([P, HALF], F32, name="bank") for r in range(ahead)]
+            for r in range(ahead):
+                archive_pass(banks[r], 0, r)
+            for r in range(8):
+                if r >= ahead:
+                    banks.append(psum.tile([P, HALF], F32, name="bank"))
+                    archive_pass(banks[r], 0, r)
+                archive_pass(banks[r], 1, r)
+                nc.scalar.activation(
+                    neg_b[h][r // 4][:, r % 4, :], banks[r][:], ACT.Identity, bias=cols[:, r : r + 1], scale=-1.0
+                )
+
+        v1 = [[None, None], [None, None]]
+        for h in range(2):
+            v1[h][0] = gather(tab[0], list1, h, U32, "v1_%d0" % h)
+        sc1 = [gather(tab_sc, list1, h, U8, "sc1_%d" % h) for h in range(2)]
+        for h in range(2):
+            v1[h][1] = gather(tab[1], list1, h, U32, "v1_%d1" % h)
+
+        wv_codes = [held([P, 2 * P], U32, "wv_codes%d" % m) for m in range(3)]
+        wv_sc = [held([P, 2 * P], U8, "wv_sc%d" % m) for m in range(3)]
+        wv_bf = [held([P, 2, 4 * P], BF16, "wv_bf%d" % m) for m in range(3)]
+        for m in range(3):
+            for b in range(2):
+                nc.gpsimd.tensor_copy(
+                    wv_bf[m][:, b, :].rearrange("p (c i t) -> p c t i", t=4, i=4),
+                    wv_raw[b][:, :, m * P : (m + 1) * P].rearrange("p t (c i) -> p c t i", i=4),
+                )
+
+        def quantize_wv():
+            for m in range(3):
+                nc.vector.quantize_mx(
+                    out=wv_codes[m][:].bitcast(FP8X4), scales=wv_sc[m][:],
+                    in_=wv_bf[m][:].rearrange("p b c -> p (b c)"),
+                )
+
+        def embed(j0, b, h_bf, at):
+            h, j = divmod(j0, HALF)
+            bank = psum.tile([P, HALF], F32, name="bank")
+            for t in range(4):
+                for a in range(2):
+                    codes, scale = w8_operand(a, 4 * b + t)
+                    nc.tensor.matmul_mx(
+                        out=bank[:, t * CHUNK : (t + 1) * CHUNK], lhsT=codes, lhsT_scale=scale,
+                        rhs=v1[h][a][:, j : j + CHUNK].bitcast(FP8X4),
+                        rhs_scale=sc1[h][TAB_ROW + 4 * a : P, j : j + CHUNK],
+                        start=(a == 0), stop=(a == 1),
+                    )
+            diff = ring.tile([P, 4, CHUNK], F32, name="diff")
+            nc.vector.tensor_tensor(
+                diff[:], bank[:].rearrange("p (t j) -> p t j", t=4), neg_b[h][b][:, :, j : j + CHUNK], ADD
+            )
+            nc.scalar.activation(
+                h_bf[:, 4 * at : 4 * (at + CHUNK)].rearrange("p (c i t) -> p c t i", t=4, i=4),
+                diff[:].rearrange("p t (c i) -> p c t i", i=4),
+                ACT.Abs,
+            )
+
+        def quantize_h(h_bf, codes, scales):
+            nc.vector.quantize_mx(out=codes[:].bitcast(FP8X4), scales=scales[:], in_=h_bf[:])
+
+        def verify(j0, width, codes, scales):
+            prob = held([P, 3, width], F32, "prob%d" % j0)
+            per_bank = HALF // width
+            for m in range(3):
+                if m % per_bank == 0:
+                    bank = psum.tile([P, HALF], F32, name="bank")
+                logits = bank[:, (m % per_bank) * width : (m % per_bank + 1) * width]
+                for b in range(2):
+                    nc.tensor.matmul_mx(
+                        out=logits, lhsT=wv_codes[m][:, b * P : (b + 1) * P].bitcast(FP8X4),
+                        lhsT_scale=wv_sc[m][:, b * P : (b + 1) * P],
+                        rhs=codes[b][:].bitcast(FP8X4), rhs_scale=scales[b][:],
+                        start=(b == 0), stop=(b == 1),
+                    )
+                nc.scalar.activation(prob[:, m, :], logits, ACT.Sigmoid, bias=cols[:, 8 + m : 9 + m])
+            nc.sync.dma_start(out.rearrange("(m p) j -> p m j", p=P)[:, :, j0 : j0 + width], prob[:])
+
+        waiting = []
+        j0 = 0
+        for width in GROUPS:
+            codes = [held([P, width], U32, "h_codes%d_%d" % (j0, b)) for b in range(2)]
+            scales = [held([P, width], U8, "h_sc%d_%d" % (j0, b)) for b in range(2)]
+            for b in range(2):
+                h_bf = held([P, 4 * width], BF16, "h_bf%d_%d" % (j0, b))
+                for at in range(0, width, CHUNK):
+                    embed(j0 + at, b, h_bf, at)
+                    for step in waiting:
+                        step()
+                    waiting = []
+                waiting.append(lambda h_bf=h_bf, c=codes[b], s=scales[b]: quantize_h(h_bf, c, s))
+                if j0 == 0 and b == 1:
+                    waiting.append(quantize_wv)
+            waiting.append(lambda j0=j0, width=width, c=codes, s=scales: verify(j0, width, c, s))
+            j0 = j0 + width
+        for step in waiting:
+            step()

@@ -33,8 +33,8 @@ def tile_list_loop_closure_vetting_kernel(
         ring = ctx.enter_context(tc.tile_pool(name="ring", bufs=4))
         psum = ctx.enter_context(tc.psum_pool(name="psum", bufs=8))
 
-        def held(shape, dtype, name):
-            return keep.tile(shape, dtype, name=name, align_bytes=64)
+        def held(shape, dtype, name, tag=None):
+            return keep.tile(shape, dtype, name=name, tag=tag or name, align_bytes=64)
 
         list1 = held([P, S // 16], U16, "list1")
         list2 = held([P, S // 16], U16, "list2")
@@ -50,16 +50,15 @@ def tile_list_loop_closure_vetting_kernel(
         ident = held([P, P], F32, "ident")
         cols = held([P, 16], F32, "cols")
         warm = held([P, 1], F32, "warm")
-        shifted = [held([P, HALF // 4], I32, "shifted%d" % h) for h in range(2)]
-        wv_raw = [held([P, 4, N], F32, "wv_raw%d" % b) for b in range(2)]
+        shifted = held([P, S // 4], I32, "shifted")
+        rows_in = held([16, P], F32, "rows_in")
 
         make_identity(nc, ident[:])
         nc.vector.memset(tab2_sc[:], 0)
-        nc.vector.memset(w8_sc_raw[:], 0)
         nc.vector.memset(rows[:], 0.0)
         nc.vector.memset(tab_sc[:], 0)
-        for h in range(2):
-            nc.vector.memset(shifted[h][:], 0)
+        nc.vector.memset(w8_sc[:], 0)
+        nc.vector.memset(shifted[:], 0)
         nc.scalar.activation(warm[:], rows[:, 0:1], ACT.Sigmoid)
 
         nc.sync.dma_start(list2[:], offs2)
@@ -78,10 +77,10 @@ def tile_list_loop_closure_vetting_kernel(
         nc.sync.dma_start(tab2[1][:], tab2_words[1].bitcast(I32))
         for b in range(2):
             nc.scalar.dma_start(
-                rows[4 * b : 4 * b + 4, :].rearrange("t (g i) -> t g i", i=8),
+                rows_in[4 * b : 4 * b + 4, :].rearrange("t (g i) -> t g i", i=8),
                 dm[512 * b : 512 * (b + 1)].rearrange("(g t i) -> t g i", t=4, i=8),
             )
-        nc.scalar.dma_start(rows[8:11, :], bv.rearrange("(m p) -> m p", p=P))
+        nc.scalar.dma_start(rows_in[8:11, :], bv.rearrange("(m p) -> m p", p=P))
         nc.sync.dma_start(list1[:], offs)
         for a in range(2):
             nc.sync.dma_start(tab[a][:], tab_words[a].rearrange("p c i -> p (c i)").bitcast(I32))
@@ -89,48 +88,48 @@ def tile_list_loop_closure_vetting_kernel(
             nc.gpsimd.dma_start(
                 tab_sc[32 * q + TAB_ROW : 32 * q + TAB_ROW + 8, :], tab_scales[:, 4 * q : 4 * q + 4, :].bitcast(I32)
             )
-        for b in range(2):
-            by_slot = wv[512 * b : 512 * (b + 1), :].rearrange("(g t i) n -> t g i n", t=4, i=8)
-            for t in range(4):
-                nc.sync.dma_start(wv_raw[b][:, t, :], by_slot[t])
 
+        nc.vector.tensor_copy(rows[0:11, :], rows_in[0:11, :])
         turned = psum.tile([P, HALF], F32, name="bank")
         nc.tensor.transpose(turned[:, 0:P], rows[:], ident[:])
         nc.scalar.copy(cols[:], turned[:, 0:16])
 
+        for q in range(4):
+            nc.vector.tensor_copy(
+                w8_sc[32 * q : 32 * q + 4, :].rearrange("p (u t g i) -> p u t g i", u=4, t=4, i=2),
+                w8_sc_raw[32 * q : 32 * q + 4, :].rearrange("p (u g t i) -> p u t g i", u=4, t=4, i=2),
+            )
         nc.vector.tensor_copy(
             w8[:].rearrange("p (u t g i) -> p u t g i", u=4, t=4, i=8),
             w8_raw[:].rearrange("p (u g t i) -> p u t g i", u=4, t=4, i=8),
-        )
-        nc.vector.tensor_copy(
-            w8_sc[:].rearrange("p (u t g i) -> p u t g i", u=4, t=4, i=2),
-            w8_sc_raw[:].rearrange("p (u g t i) -> p u t g i", u=4, t=4, i=2),
         )
 
         def half_of(offsets, h):
             return offsets[:, h * HALF // 16 : (h + 1) * HALF // 16]
 
-        def gather(window, offsets, h, dtype, name):
-            picked = held([P, HALF], dtype, name)
-            nc.vector.tensor_copy(picked[:], window[:].bitcast(dtype).indirect(half_of(offsets, h)))
-            return picked
+        def gather(picked, window, offsets, dtype):
+            nc.vector.tensor_copy(picked, window[:].bitcast(dtype).indirect(offsets))
 
         def w8_operand(a, r):
             c = slice(a * H + r * P, a * H + (r + 1) * P)
             return w8[:, c].bitcast(FP8X4), w8_sc[:].bitcast(U8)[:, c]
 
         neg_b = [[held([P, 4, HALF], F32, "neg_b%d%d" % (h, b)) for b in range(2)] for h in range(2)]
-        shift_queue = (nc.scalar, nc.gpsimd)
+        sc2 = held([P, S], U8, "sc2")
+        gather(sc2[:], tab2_sc, list2[:], U8)
+        nc.gpsimd.dma_start(shifted[0:112, :], sc2[4:116, :].bitcast(I32))
+        v2_all = held([P, 4 * HALF], U16, "v2_all", tag="tab2_sc")
         for h in range(2):
-            sc2 = gather(tab2_sc, list2, h, U8, "sc2_%d" % h)
-            shift_queue[h].dma_start(shifted[h][0:112, :], sc2[4:116, :].bitcast(I32))
-            v2 = [gather(tab2[a], list2, h, U16, "v2_%d%d" % (h, a)) for a in range(2)]
-            planes = (sc2[:], shifted[h][:].bitcast(U8))
+            v2 = [v2_all[:, (2 * h + a) * HALF : (2 * h + a + 1) * HALF] for a in range(2)]
+            for a in range(2):
+                gather(v2[a], tab2[a], half_of(list2, h), U16)
+            tokens = slice(h * HALF, (h + 1) * HALF)
+            planes = (sc2[:, tokens], shifted[:].bitcast(U8)[:, tokens])
 
             def archive_pass(bank, a, r):
                 codes, scale = w8_operand(a, r)
                 nc.tensor.matmul_mx(
-                    out=bank[:], lhsT=codes, lhsT_scale=scale, rhs=v2[a][:].bitcast(FP4X4), rhs_scale=planes[a],
+                    out=bank[:], lhsT=codes, lhsT_scale=scale, rhs=v2[a].bitcast(FP4X4), rhs_scale=planes[a],
                     start=(a == 0), stop=(a == 1),
                 )
 
@@ -147,28 +146,42 @@ def tile_list_loop_closure_vetting_kernel(
                     neg_b[h][r // 4][:, r % 4, :], banks[r][:], ACT.Identity, bias=cols[:, r : r + 1], scale=-1.0
                 )
 
-        v1 = [[None, None], [None, None]]
+        wv_raw = held([P, 8 * N], F32, "wv_raw", tag="tab2_0")
+        for b in range(2):
+            by_slot = wv[512 * b : 512 * (b + 1), :].rearrange("(g t i) n -> t g i n", t=4, i=8)
+            for t in range(4):
+                nc.sync.dma_start(wv_raw[:, (4 * b + t) * N : (4 * b + t + 1) * N], by_slot[t])
+
+        v1 = [held([P, S], U32, "v1_0", tag="tab2_1"), None]
+        gather(v1[0][:], tab[0], list1[:], U32)
+        sc1 = held([P, S], U8, "sc1")
+        gather(sc1[:], tab_sc, list1[:], U8)
+        v1[1] = held([P, S], U32, "v1_1", tag="tab_sc")
         for h in range(2):
-            v1[h][0] = gather(tab[0], list1, h, U32, "v1_%d0" % h)
-        sc1 = [gather(tab_sc, list1, h, U8, "sc1_%d" % h) for h in range(2)]
-        for h in range(2):
-            v1[h][1] = gather(tab[1], list1, h, U32, "v1_%d1" % h)
+            gather(v1[1][:, h * HALF : (h + 1) * HALF], tab[1], half_of(list1, h), U32)
 
         wv_codes = [held([P, 2 * P], U32, "wv_codes%d" % m) for m in range(3)]
         wv_sc = [held([P, 2 * P], U8, "wv_sc%d" % m) for m in range(3)]
-        wv_bf = [held([P, 2, 4 * P], BF16, "wv_bf%d" % m) for m in range(3)]
+        wv_bf = held([P, 6 * HALF], BF16, "wv_bf")
+
+        def round_wv(engine, m, b):
+            engine.tensor_copy(
+                wv_bf[:, (2 * m + b) * HALF : (2 * m + b + 1) * HALF].rearrange("p (c i t) -> p c t i", t=4, i=4),
+                wv_raw[:, 4 * b * N : 4 * (b + 1) * N].rearrange("p (t n) -> p t n", t=4)[:, :, m * P : (m + 1) * P]
+                .rearrange("p t (c i) -> p c t i", i=4),
+            )
+
         for m in range(3):
-            for b in range(2):
-                nc.gpsimd.tensor_copy(
-                    wv_bf[m][:, b, :].rearrange("p (c i t) -> p c t i", t=4, i=4),
-                    wv_raw[b][:, :, m * P : (m + 1) * P].rearrange("p t (c i) -> p c t i", i=4),
-                )
+            round_wv(nc.gpsimd, m, 0)
+        round_wv(nc.gpsimd, 2, 1)
 
         def quantize_wv():
+            for m in range(2):
+                round_wv(nc.vector, m, 1)
             for m in range(3):
                 nc.vector.quantize_mx(
                     out=wv_codes[m][:].bitcast(FP8X4), scales=wv_sc[m][:],
-                    in_=wv_bf[m][:].rearrange("p b c -> p (b c)"),
+                    in_=wv_bf[:, 2 * m * HALF : 2 * (m + 1) * HALF],
                 )
 
         def embed(j0, b, h_bf, at):
@@ -179,8 +192,8 @@ def tile_list_loop_closure_vetting_kernel(
                     codes, scale = w8_operand(a, 4 * b + t)
                     nc.tensor.matmul_mx(
                         out=bank[:, t * CHUNK : (t + 1) * CHUNK], lhsT=codes, lhsT_scale=scale,
-                        rhs=v1[h][a][:, j : j + CHUNK].bitcast(FP8X4),
-                        rhs_scale=sc1[h][TAB_ROW + 4 * a : P, j : j + CHUNK],
+                        rhs=v1[a][:, j0 : j0 + CHUNK].bitcast(FP8X4),
+                        rhs_scale=sc1[TAB_ROW + 4 * a : P, j0 : j0 + CHUNK],
                         start=(a == 0), stop=(a == 1),
                     )
             diff = ring.tile([P, 4, CHUNK], F32, name="diff")

@@ -38,20 +38,19 @@ def tile_list_loop_closure_vetting_kernel(
 
         list1 = held([P, S // 16], U16, "list1")
         list2 = held([P, S // 16], U16, "list2")
-        tab = [held([P, T], I32, "tab%d" % a) for a in range(2)]
-        tab2 = [held([P, T // 2], I32, "tab2_%d" % a) for a in range(2)]
-        tab_sc = held([P, T // 4], I32, "tab_sc")
         tab2_sc = held([P, T // 4], I32, "tab2_sc")
+        tab_sc = held([P, T // 4], I32, "tab_sc")
         w8_raw = held([P, 2 * H], I32, "w8_raw")
         w8 = held([P, 2 * H], I32, "w8")
         w8_sc_raw = held([P, 2 * H // 4], I32, "w8_sc_raw")
         w8_sc = held([P, 2 * H // 4], I32, "w8_sc")
+        rows_in = held([16, P], F32, "rows_in")
         rows = held([P, P], F32, "rows")
         ident = held([P, P], F32, "ident")
         cols = held([P, 16], F32, "cols")
         warm = held([P, 1], F32, "warm")
         shifted = held([P, S // 4], I32, "shifted")
-        rows_in = held([16, P], F32, "rows_in")
+        planes1 = held([P, S // 4], I32, "planes1")
 
         make_identity(nc, ident[:])
         nc.vector.memset(tab2_sc[:], 0)
@@ -59,40 +58,41 @@ def tile_list_loop_closure_vetting_kernel(
         nc.vector.memset(tab_sc[:], 0)
         nc.vector.memset(w8_sc[:], 0)
         nc.vector.memset(shifted[:], 0)
-        nc.scalar.activation(warm[:], rows[:, 0:1], ACT.Sigmoid)
+        nc.vector.memset(planes1[:], 0)
+        nc.scalar.activation(warm[:], ident[:, 0:1], ACT.Sigmoid)
 
-        nc.sync.dma_start(list2[:], offs2)
+        for b in range(2):
+            nc.sync.dma_start(
+                rows_in[4 * b : 4 * b + 4, :].rearrange("t (g i) -> t g i", i=8),
+                dm[512 * b : 512 * (b + 1)].rearrange("(g t i) -> t g i", t=4, i=8),
+            )
+        nc.sync.dma_start(rows_in[8:11, :], bv.rearrange("(m p) -> m p", p=P))
+        for q in range(4):
+            nc.sync.dma_start(
+                w8_sc_raw[32 * q : 32 * q + 4, :].rearrange("r (a c) -> r a c", a=2),
+                w8_scales[:, 4 * q : 4 * q + 4, :].rearrange("a r c -> r a c").bitcast(I32),
+            )
         nc.sync.dma_start(
             w8_raw[:].rearrange("p (a c) -> p a c", a=2),
             w8_words.rearrange("a p c i -> p a (c i)").bitcast(I32),
         )
-        nc.sync.dma_start(tab2[0][:], tab2_words[0].bitcast(I32))
-        for q in range(4):
-            nc.gpsimd.dma_start(tab2_sc[32 * q : 32 * q + 8, :], tab2_scales[:, 4 * q : 4 * q + 4, :].bitcast(I32))
-        for q in range(4):
-            nc.scalar.dma_start(
-                w8_sc_raw[32 * q : 32 * q + 4, :].rearrange("r (a c) -> r a c", a=2),
-                w8_scales[:, 4 * q : 4 * q + 4, :].rearrange("a r c -> r a c").bitcast(I32),
-            )
-        nc.sync.dma_start(tab2[1][:], tab2_words[1].bitcast(I32))
-        for b in range(2):
-            nc.scalar.dma_start(
-                rows_in[4 * b : 4 * b + 4, :].rearrange("t (g i) -> t g i", i=8),
-                dm[512 * b : 512 * (b + 1)].rearrange("(g t i) -> t g i", t=4, i=8),
-            )
-        nc.scalar.dma_start(rows_in[8:11, :], bv.rearrange("(m p) -> m p", p=P))
+        nc.sync.dma_start(list2[:], offs2)
         nc.sync.dma_start(list1[:], offs)
         for a in range(2):
-            nc.sync.dma_start(tab[a][:], tab_words[a].rearrange("p c i -> p (c i)").bitcast(I32))
-        for q in range(4):
-            nc.gpsimd.dma_start(
-                tab_sc[32 * q + TAB_ROW : 32 * q + TAB_ROW + 8, :], tab_scales[:, 4 * q : 4 * q + 4, :].bitcast(I32)
-            )
+            for q in range(4):
+                at = 32 * q + 4 * a
+                nc.sync.dma_start(tab2_sc[at : at + 4, :], tab2_scales[a, 4 * q : 4 * q + 4, :].bitcast(I32))
+
+        nc.sync.dma_start(tab_sc[0:32, :], tab_scales.rearrange("a q c -> (a q) c").bitcast(I32))
 
         nc.vector.tensor_copy(rows[0:11, :], rows_in[0:11, :])
         turned = psum.tile([P, HALF], F32, name="bank")
         nc.tensor.transpose(turned[:, 0:P], rows[:], ident[:])
         nc.scalar.copy(cols[:], turned[:, 0:16])
+
+        tab2 = [held([P, T // 2], I32, "tab2_%d" % a, tag=("rows_in", "rows")[a]) for a in range(2)]
+        for a in range(2):
+            nc.sync.dma_start(tab2[a][:], tab2_words[a].bitcast(I32))
 
         for q in range(4):
             nc.vector.tensor_copy(
@@ -117,8 +117,15 @@ def tile_list_loop_closure_vetting_kernel(
         neg_b = [[held([P, 4, HALF], F32, "neg_b%d%d" % (h, b)) for b in range(2)] for h in range(2)]
         sc2 = held([P, S], U8, "sc2")
         gather(sc2[:], tab2_sc, list2[:], U8)
-        nc.gpsimd.dma_start(shifted[0:112, :], sc2[4:116, :].bitcast(I32))
-        v2_all = held([P, 4 * HALF], U16, "v2_all", tag="tab2_sc")
+        nc.sync.dma_start(shifted[0:112, :], sc2[4:116, :].bitcast(I32))
+
+        def load_tab(a, tag):
+            words = held([P, T], I32, "tab%d" % a, tag=tag)
+            nc.sync.dma_start(words[:], tab_words[a].rearrange("p c i -> p (c i)").bitcast(I32))
+            return words
+
+        tab = [load_tab(0, "tab2_sc")]
+        v2_all = held([P, 4 * HALF], U16, "v2_all")
         for h in range(2):
             v2 = [v2_all[:, (2 * h + a) * HALF : (2 * h + a + 1) * HALF] for a in range(2)]
             for a in range(2):
@@ -146,38 +153,40 @@ def tile_list_loop_closure_vetting_kernel(
                     neg_b[h][r // 4][:, r % 4, :], banks[r][:], ACT.Identity, bias=cols[:, r : r + 1], scale=-1.0
                 )
 
-        wv_raw = held([P, 8 * N], F32, "wv_raw", tag="tab2_0")
+        tab.append(load_tab(1, "rows_in"))
+        sc1 = held([P, S], U8, "sc1", tag="rows")
+        gather(sc1[:], tab_sc, list1[:], U8)
+        for a in range(2):
+            for q in range(4):
+                row, at = 16 * a + 4 * q, 32 * q + TAB_ROW + 4 * a
+                nc.sync.dma_start(planes1[at : at + 4, :], sc1[row : row + 4, :].bitcast(I32))
+        v1_all = held([P, 2 * S], U32, "v1_all", tag="tab_sc")
+        v1 = [v1_all[:, a * S : (a + 1) * S] for a in range(2)]
+        gather(v1[0], tab[0], list1[:], U32)
+        for h in range(2):
+            gather(v1[1][:, h * HALF : (h + 1) * HALF], tab[1], half_of(list1, h), U32)
+
+        wv_raw = held([P, 8 * N], F32, "wv_raw", tag="tab2_sc")
         for b in range(2):
             by_slot = wv[512 * b : 512 * (b + 1), :].rearrange("(g t i) n -> t g i n", t=4, i=8)
             for t in range(4):
                 nc.sync.dma_start(wv_raw[:, (4 * b + t) * N : (4 * b + t + 1) * N], by_slot[t])
 
-        v1 = [held([P, S], U32, "v1_0", tag="tab2_1"), None]
-        gather(v1[0][:], tab[0], list1[:], U32)
-        sc1 = held([P, S], U8, "sc1")
-        gather(sc1[:], tab_sc, list1[:], U8)
-        v1[1] = held([P, S], U32, "v1_1", tag="tab_sc")
-        for h in range(2):
-            gather(v1[1][:, h * HALF : (h + 1) * HALF], tab[1], half_of(list1, h), U32)
-
         wv_codes = [held([P, 2 * P], U32, "wv_codes%d" % m) for m in range(3)]
         wv_sc = [held([P, 2 * P], U8, "wv_sc%d" % m) for m in range(3)]
         wv_bf = held([P, 6 * HALF], BF16, "wv_bf")
 
-        def round_wv(engine, m, b):
-            engine.tensor_copy(
+        def round_wv(copy, m, b):
+            copy(
                 wv_bf[:, (2 * m + b) * HALF : (2 * m + b + 1) * HALF].rearrange("p (c i t) -> p c t i", t=4, i=4),
                 wv_raw[:, 4 * b * N : 4 * (b + 1) * N].rearrange("p (t n) -> p t n", t=4)[:, :, m * P : (m + 1) * P]
                 .rearrange("p t (c i) -> p c t i", i=4),
             )
 
-        for m in range(3):
-            round_wv(nc.gpsimd, m, 0)
-        round_wv(nc.gpsimd, 2, 1)
-
         def quantize_wv():
-            for m in range(2):
-                round_wv(nc.vector, m, 1)
+            for m in range(3):
+                round_wv(nc.scalar.copy, m, 0)
+                round_wv(nc.vector.tensor_copy, m, 1)
             for m in range(3):
                 nc.vector.quantize_mx(
                     out=wv_codes[m][:].bitcast(FP8X4), scales=wv_sc[m][:],
@@ -193,7 +202,7 @@ def tile_list_loop_closure_vetting_kernel(
                     nc.tensor.matmul_mx(
                         out=bank[:, t * CHUNK : (t + 1) * CHUNK], lhsT=codes, lhsT_scale=scale,
                         rhs=v1[a][:, j0 : j0 + CHUNK].bitcast(FP8X4),
-                        rhs_scale=sc1[TAB_ROW + 4 * a : P, j0 : j0 + CHUNK],
+                        rhs_scale=planes1[:].bitcast(U8)[TAB_ROW + 4 * a : P, j0 : j0 + CHUNK],
                         start=(a == 0), stop=(a == 1),
                     )
             diff = ring.tile([P, 4, CHUNK], F32, name="diff")
@@ -239,7 +248,7 @@ def tile_list_loop_closure_vetting_kernel(
                         step()
                     waiting = []
                 waiting.append(lambda h_bf=h_bf, c=codes[b], s=scales[b]: quantize_h(h_bf, c, s))
-                if j0 == 0 and b == 1:
+                if j0 == 0 and b == 0:
                     waiting.append(quantize_wv)
             waiting.append(lambda j0=j0, width=width, c=codes, s=scales: verify(j0, width, c, s))
             j0 = j0 + width

@@ -21,7 +21,7 @@ P = 128
 HALF = 512
 CHUNK = 128
 GROUPS = (512, 256, 128, 128)
-TAB_ROW = 8
+LAG = 2
 
 
 def tile_list_loop_closure_vetting_kernel(
@@ -44,65 +44,67 @@ def tile_list_loop_closure_vetting_kernel(
         w8 = held([P, 2 * H], I32, "w8")
         w8_sc_raw = held([P, 2 * H // 4], I32, "w8_sc_raw")
         w8_sc = held([P, 2 * H // 4], I32, "w8_sc")
-        rows_in = held([16, P], F32, "rows_in")
-        rows = held([P, P], F32, "rows")
         ident = held([P, P], F32, "ident")
         cols = held([P, 16], F32, "cols")
         warm = held([P, 1], F32, "warm")
         shifted = held([P, S // 4], I32, "shifted")
         planes1 = held([P, S // 4], I32, "planes1")
 
-        make_identity(nc, ident[:])
-        nc.vector.memset(tab2_sc[:], 0)
-        nc.vector.memset(rows[:], 0.0)
-        nc.vector.memset(tab_sc[:], 0)
-        nc.vector.memset(w8_sc[:], 0)
-        nc.vector.memset(shifted[:], 0)
-        nc.vector.memset(planes1[:], 0)
-        nc.scalar.activation(warm[:], ident[:, 0:1], ACT.Sigmoid)
-
+        rows = held([P, P], F32, "rows")
+        nc.gpsimd.memset(rows[:], 0.0)
         for b in range(2):
-            nc.sync.dma_start(
-                rows_in[4 * b : 4 * b + 4, :].rearrange("t (g i) -> t g i", i=8),
+            nc.gpsimd.dma_start(
+                rows[4 * b : 4 * b + 4, :].rearrange("t (g i) -> t g i", i=8),
                 dm[512 * b : 512 * (b + 1)].rearrange("(g t i) -> t g i", t=4, i=8),
             )
-        nc.sync.dma_start(rows_in[8:11, :], bv.rearrange("(m p) -> m p", p=P))
-        for q in range(4):
-            nc.sync.dma_start(
-                w8_sc_raw[32 * q : 32 * q + 4, :].rearrange("r (a c) -> r a c", a=2),
-                w8_scales[:, 4 * q : 4 * q + 4, :].rearrange("a r c -> r a c").bitcast(I32),
-            )
+        nc.gpsimd.dma_start(rows[8:11, :], bv.rearrange("(m p) -> m p", p=P))
+        make_identity(nc, ident[:])
+        zero = held([P, 1], F32, "zero")
+        nc.vector.memset(zero[:], 0.0)
+        nc.vector.memset(tab2_sc[:], 0)
+        nc.vector.memset(shifted[:], 0)
+        nc.vector.memset(planes1[:], 0)
+        nc.vector.memset(tab_sc[:], 0)
+        nc.vector.memset(w8_sc_raw[:], 0)
+        nc.scalar.activation(warm[:], zero[:], ACT.Sigmoid)
+
+        nc.sync.dma_start(list2[:], offs2)
+        nc.sync.dma_start(list1[:], offs)
         nc.sync.dma_start(
             w8_raw[:].rearrange("p (a c) -> p a c", a=2),
             w8_words.rearrange("a p c i -> p a (c i)").bitcast(I32),
         )
-        nc.sync.dma_start(list2[:], offs2)
-        nc.sync.dma_start(list1[:], offs)
-        for a in range(2):
-            for q in range(4):
-                at = 32 * q + 4 * a
-                nc.sync.dma_start(tab2_sc[at : at + 4, :], tab2_scales[a, 4 * q : 4 * q + 4, :].bitcast(I32))
+        for r in range(4):
+            nc.sync.dma_start(tab2_sc[r:P:32, :], tab2_scales[0, r:16:4, :].bitcast(I32))
+        nc.sync.dma_start(tab2_sc[4:P:8, :], tab2_scales[1].bitcast(I32))
 
-        nc.sync.dma_start(tab_sc[0:32, :], tab_scales.rearrange("a q c -> (a q) c").bitcast(I32))
+        def load_tab2(a, tag):
+            words = held([P, T // 2], I32, "tab2_%d" % a, tag=tag)
+            nc.sync.dma_start(words[:], tab2_words[a].bitcast(I32))
+            return words
 
-        nc.vector.tensor_copy(rows[0:11, :], rows_in[0:11, :])
-        turned = psum.tile([P, HALF], F32, name="bank")
-        nc.tensor.transpose(turned[:, 0:P], rows[:], ident[:])
-        nc.scalar.copy(cols[:], turned[:, 0:16])
-
-        tab2 = [held([P, T // 2], I32, "tab2_%d" % a, tag=("rows_in", "rows")[a]) for a in range(2)]
-        for a in range(2):
-            nc.sync.dma_start(tab2[a][:], tab2_words[a].bitcast(I32))
-
-        for q in range(4):
-            nc.vector.tensor_copy(
-                w8_sc[32 * q : 32 * q + 4, :].rearrange("p (u t g i) -> p u t g i", u=4, t=4, i=2),
-                w8_sc_raw[32 * q : 32 * q + 4, :].rearrange("p (u g t i) -> p u t g i", u=4, t=4, i=2),
+        tab2 = [load_tab2(0, "warm")]
+        for r in range(4):
+            nc.sync.dma_start(
+                w8_sc_raw[r:P:32, :].rearrange("q (a c) -> q a c", a=2),
+                w8_scales[:, r:16:4, :].rearrange("a q c -> q a c").bitcast(I32),
             )
+        for a in range(2):
+            nc.sync.dma_start(tab_sc[4 * a : P : 8, :], tab_scales[a].bitcast(I32))
+
         nc.vector.tensor_copy(
             w8[:].rearrange("p (u t g i) -> p u t g i", u=4, t=4, i=8),
             w8_raw[:].rearrange("p (u g t i) -> p u t g i", u=4, t=4, i=8),
         )
+        nc.vector.tensor_copy(
+            w8_sc[:].rearrange("p (u t g i) -> p u t g i", u=4, t=4, i=2),
+            w8_sc_raw[:].rearrange("p (u g t i) -> p u t g i", u=4, t=4, i=2),
+        )
+        tab2.append(load_tab2(1, "w8_raw"))
+
+        turned = psum.tile([P, HALF], F32, name="bank")
+        nc.tensor.transpose(turned[:, 0:P], rows[:], ident[:])
+        nc.scalar.copy(cols[:], turned[:, 0:16])
 
         def half_of(offsets, h):
             return offsets[:, h * HALF // 16 : (h + 1) * HALF // 16]
@@ -117,7 +119,8 @@ def tile_list_loop_closure_vetting_kernel(
         neg_b = [[held([P, 4, HALF], F32, "neg_b%d%d" % (h, b)) for b in range(2)] for h in range(2)]
         sc2 = held([P, S], U8, "sc2")
         gather(sc2[:], tab2_sc, list2[:], U8)
-        nc.sync.dma_start(shifted[0:112, :], sc2[4:116, :].bitcast(I32))
+        for r in range(4):
+            nc.sync.dma_start(shifted[r:P:32, :], sc2[8 * r + 4 : P : 32, :].bitcast(I32))
 
         def load_tab(a, tag):
             words = held([P, T], I32, "tab%d" % a, tag=tag)
@@ -125,9 +128,8 @@ def tile_list_loop_closure_vetting_kernel(
             return words
 
         tab = [load_tab(0, "tab2_sc")]
-        v2_all = held([P, 4 * HALF], U16, "v2_all")
         for h in range(2):
-            v2 = [v2_all[:, (2 * h + a) * HALF : (2 * h + a + 1) * HALF] for a in range(2)]
+            v2 = [held([P, HALF], U16, "v2_%d%d" % (h, a))[:] for a in range(2)]
             for a in range(2):
                 gather(v2[a], tab2[a], half_of(list2, h), U16)
             tokens = slice(h * HALF, (h + 1) * HALF)
@@ -153,13 +155,11 @@ def tile_list_loop_closure_vetting_kernel(
                     neg_b[h][r // 4][:, r % 4, :], banks[r][:], ACT.Identity, bias=cols[:, r : r + 1], scale=-1.0
                 )
 
-        tab.append(load_tab(1, "rows_in"))
-        sc1 = held([P, S], U8, "sc1", tag="rows")
+        tab.append(load_tab(1, "warm"))
+        sc1 = held([P, S], U8, "sc1", tag="w8_raw")
         gather(sc1[:], tab_sc, list1[:], U8)
-        for a in range(2):
-            for q in range(4):
-                row, at = 16 * a + 4 * q, 32 * q + TAB_ROW + 4 * a
-                nc.sync.dma_start(planes1[at : at + 4, :], sc1[row : row + 4, :].bitcast(I32))
+        for r in range(4):
+            nc.sync.dma_start(planes1[r : r + 104 : 4, :], sc1[8 * r : 8 * r + 104 : 4, :].bitcast(I32))
         v1_all = held([P, 2 * S], U32, "v1_all", tag="tab_sc")
         v1 = [v1_all[:, a * S : (a + 1) * S] for a in range(2)]
         gather(v1[0], tab[0], list1[:], U32)
@@ -193,7 +193,7 @@ def tile_list_loop_closure_vetting_kernel(
                     in_=wv_bf[:, 2 * m * HALF : 2 * (m + 1) * HALF],
                 )
 
-        def embed(j0, b, h_bf, at):
+        def embed(j0, b, diff):
             h, j = divmod(j0, HALF)
             bank = psum.tile([P, HALF], F32, name="bank")
             for t in range(4):
@@ -202,15 +202,16 @@ def tile_list_loop_closure_vetting_kernel(
                     nc.tensor.matmul_mx(
                         out=bank[:, t * CHUNK : (t + 1) * CHUNK], lhsT=codes, lhsT_scale=scale,
                         rhs=v1[a][:, j0 : j0 + CHUNK].bitcast(FP8X4),
-                        rhs_scale=planes1[:].bitcast(U8)[TAB_ROW + 4 * a : P, j0 : j0 + CHUNK],
+                        rhs_scale=planes1[:].bitcast(U8)[4 * a : P, j0 : j0 + CHUNK],
                         start=(a == 0), stop=(a == 1),
                     )
-            diff = ring.tile([P, 4, CHUNK], F32, name="diff")
             nc.vector.tensor_tensor(
-                diff[:], bank[:].rearrange("p (t j) -> p t j", t=4), neg_b[h][b][:, :, j : j + CHUNK], ADD
+                diff, bank[:].rearrange("p (t j) -> p t j", t=4), neg_b[h][b][:, :, j : j + CHUNK], ADD
             )
+
+        def magnitude(h_bf, diff):
             nc.scalar.activation(
-                h_bf[:, 4 * at : 4 * (at + CHUNK)].rearrange("p (c i t) -> p c t i", t=4, i=4),
+                h_bf.rearrange("p (c i t) -> p c t i", t=4, i=4),
                 diff[:].rearrange("p t (c i) -> p c t i", i=4),
                 ACT.Abs,
             )
@@ -220,11 +221,9 @@ def tile_list_loop_closure_vetting_kernel(
 
         def verify(j0, width, codes, scales):
             prob = held([P, 3, width], F32, "prob%d" % j0)
-            per_bank = HALF // width
             for m in range(3):
-                if m % per_bank == 0:
-                    bank = psum.tile([P, HALF], F32, name="bank")
-                logits = bank[:, (m % per_bank) * width : (m % per_bank + 1) * width]
+                bank = psum.tile([P, HALF], F32, name="bank")
+                logits = bank[:, 0:width]
                 for b in range(2):
                     nc.tensor.matmul_mx(
                         out=logits, lhsT=wv_codes[m][:, b * P : (b + 1) * P].bitcast(FP8X4),
@@ -236,21 +235,29 @@ def tile_list_loop_closure_vetting_kernel(
             nc.sync.dma_start(out.rearrange("(m p) j -> p m j", p=P)[:, :, j0 : j0 + width], prob[:])
 
         waiting = []
+        done = 0
         j0 = 0
         for width in GROUPS:
             codes = [held([P, width], U32, "h_codes%d_%d" % (j0, b)) for b in range(2)]
             scales = [held([P, width], U8, "h_sc%d_%d" % (j0, b)) for b in range(2)]
             for b in range(2):
                 h_bf = held([P, 4 * width], BF16, "h_bf%d_%d" % (j0, b))
+                span = min(width, 2 * CHUNK)
                 for at in range(0, width, CHUNK):
-                    embed(j0 + at, b, h_bf, at)
-                    for step in waiting:
-                        step()
-                    waiting = []
-                waiting.append(lambda h_bf=h_bf, c=codes[b], s=scales[b]: quantize_h(h_bf, c, s))
-                if j0 == 0 and b == 0:
-                    waiting.append(quantize_wv)
-            waiting.append(lambda j0=j0, width=width, c=codes, s=scales: verify(j0, width, c, s))
+                    if at % span == 0:
+                        diff = ring.tile([P, 4, span], F32, name="diff")
+                    embed(j0 + at, b, diff[:, :, at % span : at % span + CHUNK])
+                    if (at + CHUNK) % span == 0:
+                        magnitude(h_bf[:, 4 * (at + CHUNK - span) : 4 * (at + CHUNK)], diff)
+                    done = done + 1
+                    for due, step in waiting:
+                        if due == done:
+                            step()
+                waiting.append((done + LAG, lambda h_bf=h_bf, c=codes[b], s=scales[b]: quantize_h(h_bf, c, s)))
+                if j0 == 0 and b == 1:
+                    waiting.append((done + 1, quantize_wv))
+            waiting.append((done + LAG, lambda j0=j0, width=width, c=codes, s=scales: verify(j0, width, c, s)))
             j0 = j0 + width
-        for step in waiting:
-            step()
+        for due, step in waiting:
+            if due > done:
+                step()

@@ -15,12 +15,14 @@ U8 = mybir.dt.uint8
 FP8X4 = mybir.dt.float8_e4m3fn_x4
 FP4X4 = mybir.dt.float4_e2m1fn_x4
 ACT = mybir.ActivationFunctionType
-ADD = mybir.AluOpType.add
+ALU = mybir.AluOpType
 
 P = 128
 HALF = 512
-CHUNK = 128
-GROUPS = (512, 256, 128, 128)
+BANK = 512
+ROWS = slice(96, 128)
+GROUPS = (256, 256, 256, 128, 128)
+AHEAD = 4
 LAG = 2
 
 
@@ -38,19 +40,23 @@ def tile_list_loop_closure_vetting_kernel(
 
         list1 = held([P, S // 16], U16, "list1")
         list2 = held([P, S // 16], U16, "list2")
-        tab2_sc = held([P, T // 4], I32, "tab2_sc")
-        tab_sc = held([P, T // 4], I32, "tab_sc")
+        win2 = held([P, T // 4], I32, "win2")
+        planes1 = held([P, S // 4], I32, "planes1")
+        w8_sc_raw = held([P, H // 4], I32, "w8_sc_raw")
         w8_raw = held([P, 2 * H], I32, "w8_raw")
         w8 = held([P, 2 * H], I32, "w8")
-        w8_sc_raw = held([P, 2 * H // 4], I32, "w8_sc_raw")
-        w8_sc = held([P, 2 * H // 4], I32, "w8_sc")
+        planes = [held([P, 2 * S // 4], I32, "plane_pass%d" % a) for a in range(2)]
         ident = held([P, P], F32, "ident")
         cols = held([P, 16], F32, "cols")
-        warm = held([P, 1], F32, "warm")
-        shifted = held([P, S // 4], I32, "shifted")
-        planes1 = held([P, S // 4], I32, "planes1")
-
         rows = held([P, P], F32, "rows")
+        warm = held([P, 1], F32, "warm")
+        zero = held([P, 1], F32, "zero")
+
+        def scale_rows(scales):
+            return scales.rearrange("a q c -> (a q) c").bitcast(I32)
+
+        for a in range(2):
+            nc.gpsimd.memset(planes[a][:], 0)
         nc.gpsimd.memset(rows[:], 0.0)
         for b in range(2):
             nc.gpsimd.dma_start(
@@ -59,52 +65,32 @@ def tile_list_loop_closure_vetting_kernel(
             )
         nc.gpsimd.dma_start(rows[8:11, :], bv.rearrange("(m p) -> m p", p=P))
         make_identity(nc, ident[:])
-        zero = held([P, 1], F32, "zero")
-        nc.vector.memset(zero[:], 0.0)
-        nc.vector.memset(tab2_sc[:], 0)
-        nc.vector.memset(shifted[:], 0)
-        nc.vector.memset(planes1[:], 0)
-        nc.vector.memset(tab_sc[:], 0)
-        nc.vector.memset(w8_sc_raw[:], 0)
-        nc.scalar.activation(warm[:], zero[:], ACT.Sigmoid)
+        nc.gpsimd.memset(planes1[:], 0)
 
-        nc.sync.dma_start(list2[:], offs2)
-        nc.sync.dma_start(list1[:], offs)
-        nc.sync.dma_start(
-            w8_raw[:].rearrange("p (a c) -> p a c", a=2),
-            w8_words.rearrange("a p c i -> p a (c i)").bitcast(I32),
-        )
-        for r in range(4):
-            nc.sync.dma_start(tab2_sc[r:P:32, :], tab2_scales[0, r:16:4, :].bitcast(I32))
-        nc.sync.dma_start(tab2_sc[4:P:8, :], tab2_scales[1].bitcast(I32))
+        nc.vector.memset(zero[:], 0.0)
+        nc.vector.memset(win2[0:96, :], 0)
+        nc.scalar.activation(warm[:], zero[:], ACT.Sigmoid)
 
         def load_tab2(a, tag):
             words = held([P, T // 2], I32, "tab2_%d" % a, tag=tag)
             nc.sync.dma_start(words[:], tab2_words[a].bitcast(I32))
             return words
 
-        tab2 = [load_tab2(0, "warm")]
-        for r in range(4):
-            nc.sync.dma_start(
-                w8_sc_raw[r:P:32, :].rearrange("q (a c) -> q a c", a=2),
-                w8_scales[:, r:16:4, :].rearrange("a q c -> q a c").bitcast(I32),
-            )
-        for a in range(2):
-            nc.sync.dma_start(tab_sc[4 * a : P : 8, :], tab_scales[a].bitcast(I32))
+        def load_tab(a, tag):
+            words = held([P, T], I32, "tab%d" % a, tag=tag)
+            nc.sync.dma_start(words[:], tab_words[a].rearrange("p c i -> p (c i)").bitcast(I32))
+            return words
 
-        nc.vector.tensor_copy(
-            w8[:].rearrange("p (u t g i) -> p u t g i", u=4, t=4, i=8),
-            w8_raw[:].rearrange("p (u g t i) -> p u t g i", u=4, t=4, i=8),
+        nc.sync.dma_start(list2[:], offs2)
+        nc.sync.dma_start(win2[ROWS, :], scale_rows(tab2_scales))
+        nc.sync.dma_start(w8_sc_raw[ROWS, :], scale_rows(w8_scales))
+        nc.sync.dma_start(list1[:], offs)
+        tab2 = [load_tab2(0, "tab2_0")]
+        nc.sync.dma_start(
+            w8_raw[:].rearrange("p (a c) -> p a c", a=2),
+            w8_words.rearrange("a p c i -> p a (c i)").bitcast(I32),
         )
-        nc.vector.tensor_copy(
-            w8_sc[:].rearrange("p (u t g i) -> p u t g i", u=4, t=4, i=2),
-            w8_sc_raw[:].rearrange("p (u g t i) -> p u t g i", u=4, t=4, i=2),
-        )
-        tab2.append(load_tab2(1, "w8_raw"))
-
-        turned = psum.tile([P, HALF], F32, name="bank")
-        nc.tensor.transpose(turned[:, 0:P], rows[:], ident[:])
-        nc.scalar.copy(cols[:], turned[:, 0:16])
+        stage = held([P, 2 * S // 4], I32, "stage")
 
         def half_of(offsets, h):
             return offsets[:, h * HALF // 16 : (h + 1) * HALF // 16]
@@ -112,106 +98,129 @@ def tile_list_loop_closure_vetting_kernel(
         def gather(picked, window, offsets, dtype):
             nc.vector.tensor_copy(picked, window[:].bitcast(dtype).indirect(offsets))
 
+        sc2 = held([P, S], U8, "sc2")
+        gather(sc2[:], win2, list2[:], U8)
+        nc.vector.tensor_copy(
+            stage[ROWS, 0:256].rearrange("p (u t g i) -> p u t g i", u=2, t=4, i=2),
+            w8_sc_raw[ROWS, :].rearrange("p (u g t i) -> p u t g i", u=2, t=4, i=2),
+        )
+        nc.vector.tensor_copy(stage[ROWS, 256:512], sc2[ROWS, :].bitcast(I32))
+
+        def move(n):
+            a, r = divmod(n, 4)
+            first = 96 + 16 * a + r
+            nc.sync.dma_start(planes[a][r:P:32, :], stage[first : first + 13 : 4, :])
+
+        for n in range(6):
+            move(n)
+        tab2.append(load_tab2(1, "sc2"))
+        for n in range(6, 8):
+            move(n)
+        win1 = held([P, T // 4], I32, "win1", tag="win2")
+        nc.gpsimd.memset(win1[:], 0)
+        nc.sync.dma_start(win1[0:P:4, :], tab_scales.rearrange("a q c -> q a c").bitcast(I32))
+
+        turned = psum.tile([P, BANK], F32, name="bank")
+        nc.tensor.transpose(turned[:, 0:P], rows[:], ident[:])
+        nc.scalar.copy(cols[:], turned[:, 0:16])
+
         def w8_operand(a, r):
-            c = slice(a * H + r * P, a * H + (r + 1) * P)
-            return w8[:, c].bitcast(FP8X4), w8_sc[:].bitcast(U8)[:, c]
+            return (
+                w8[:, a * H + r * P : a * H + (r + 1) * P].bitcast(FP8X4),
+                planes[a][:].bitcast(U8)[:, r * P : (r + 1) * P],
+            )
+
+        def pick2(a, h):
+            picked = held([P, HALF], U16, "v2_%d%d" % (h, a))
+            gather(picked[:], tab2[a], half_of(list2, h), U16)
+            return picked
 
         neg_b = [[held([P, 4, HALF], F32, "neg_b%d%d" % (h, b)) for b in range(2)] for h in range(2)]
-        sc2 = held([P, S], U8, "sc2")
-        gather(sc2[:], tab2_sc, list2[:], U8)
-        for r in range(4):
-            nc.sync.dma_start(shifted[r:P:32, :], sc2[8 * r + 4 : P : 32, :].bitcast(I32))
 
-        def load_tab(a, tag):
-            words = held([P, T], I32, "tab%d" % a, tag=tag)
-            nc.sync.dma_start(words[:], tab_words[a].rearrange("p c i -> p (c i)").bitcast(I32))
-            return words
-
-        tab = [load_tab(0, "tab2_sc")]
-        for h in range(2):
-            v2 = [held([P, HALF], U16, "v2_%d%d" % (h, a))[:] for a in range(2)]
-            for a in range(2):
-                gather(v2[a], tab2[a], half_of(list2, h), U16)
-            tokens = slice(h * HALF, (h + 1) * HALF)
-            planes = (sc2[:, tokens], shifted[:].bitcast(U8)[:, tokens])
-
+        def archive(h, v2, ahead):
             def archive_pass(bank, a, r):
                 codes, scale = w8_operand(a, r)
                 nc.tensor.matmul_mx(
-                    out=bank[:], lhsT=codes, lhsT_scale=scale, rhs=v2[a].bitcast(FP4X4), rhs_scale=planes[a],
+                    out=bank[:], lhsT=codes, lhsT_scale=scale, rhs=v2[a][:].bitcast(FP4X4),
+                    rhs_scale=planes[a][:].bitcast(U8)[:, S + h * HALF : S + (h + 1) * HALF],
                     start=(a == 0), stop=(a == 1),
                 )
 
-            ahead = 4 if h == 0 else 0
-            banks = [psum.tile([P, HALF], F32, name="bank") for r in range(ahead)]
+            banks = [psum.tile([P, BANK], F32, name="bank") for r in range(ahead)]
             for r in range(ahead):
                 archive_pass(banks[r], 0, r)
             for r in range(8):
                 if r >= ahead:
-                    banks.append(psum.tile([P, HALF], F32, name="bank"))
+                    banks.append(psum.tile([P, BANK], F32, name="bank"))
                     archive_pass(banks[r], 0, r)
                 archive_pass(banks[r], 1, r)
                 nc.scalar.activation(
                     neg_b[h][r // 4][:, r % 4, :], banks[r][:], ACT.Identity, bias=cols[:, r : r + 1], scale=-1.0
                 )
 
-        tab.append(load_tab(1, "warm"))
-        sc1 = held([P, S], U8, "sc1", tag="w8_raw")
-        gather(sc1[:], tab_sc, list1[:], U8)
+        first0, second0 = pick2(0, 0), pick2(0, 1)
+        tab = [load_tab(0, "tab2_0")]
+        nc.vector.tensor_copy(
+            w8[:].rearrange("p (u t g i) -> p u t g i", u=4, t=4, i=8),
+            w8_raw[:].rearrange("p (u g t i) -> p u t g i", u=4, t=4, i=8),
+        )
+        tab.append(load_tab(1, "w8_raw"))
+        first1, second1 = pick2(1, 0), pick2(1, 1)
+        sc1 = held([P, S], U8, "sc1", tag="sc2")
+        gather(sc1[:], win1, list1[:], U8)
         for r in range(4):
             nc.sync.dma_start(planes1[r : r + 104 : 4, :], sc1[8 * r : 8 * r + 104 : 4, :].bitcast(I32))
-        v1_all = held([P, 2 * S], U32, "v1_all", tag="tab_sc")
-        v1 = [v1_all[:, a * S : (a + 1) * S] for a in range(2)]
-        gather(v1[0], tab[0], list1[:], U32)
+        archive(0, [first0, first1], AHEAD)
+        archive(1, [second0, second1], 0)
+
+        v1 = [held([P, S], U32, "v1_%d" % a) for a in range(2)]
+        gather(v1[0][:], tab[0], list1[:], U32)
         for h in range(2):
             gather(v1[1][:, h * HALF : (h + 1) * HALF], tab[1], half_of(list1, h), U32)
 
-        wv_raw = held([P, 8 * N], F32, "wv_raw", tag="tab2_sc")
+        wv_raw = held([P, 8 * N], F32, "wv_raw", tag="win2")
         for b in range(2):
             by_slot = wv[512 * b : 512 * (b + 1), :].rearrange("(g t i) n -> t g i n", t=4, i=8)
             for t in range(4):
                 nc.sync.dma_start(wv_raw[:, (4 * b + t) * N : (4 * b + t + 1) * N], by_slot[t])
 
-        wv_codes = [held([P, 2 * P], U32, "wv_codes%d" % m) for m in range(3)]
-        wv_sc = [held([P, 2 * P], U8, "wv_sc%d" % m) for m in range(3)]
+        wv_codes = held([P, 2 * N], U32, "wv_codes")
+        wv_sc = held([P, 2 * N], U8, "wv_sc")
         wv_bf = held([P, 6 * HALF], BF16, "wv_bf")
 
-        def round_wv(copy, m, b):
-            copy(
-                wv_bf[:, (2 * m + b) * HALF : (2 * m + b + 1) * HALF].rearrange("p (c i t) -> p c t i", t=4, i=4),
-                wv_raw[:, 4 * b * N : 4 * (b + 1) * N].rearrange("p (t n) -> p t n", t=4)[:, :, m * P : (m + 1) * P]
-                .rearrange("p t (c i) -> p c t i", i=4),
-            )
-
         def quantize_wv():
-            for m in range(3):
-                round_wv(nc.scalar.copy, m, 0)
-                round_wv(nc.vector.tensor_copy, m, 1)
-            for m in range(3):
+            for b in range(2):
+                nc.vector.tensor_copy(
+                    wv_bf[:, 4 * b * N : 4 * (b + 1) * N].rearrange("p (c i t) -> p c t i", t=4, i=4),
+                    wv_raw[:, 4 * b * N : 4 * (b + 1) * N].rearrange("p (t c i) -> p c t i", t=4, i=4),
+                )
+            for c0, c1 in ((0, 256), (256, 768)):
                 nc.vector.quantize_mx(
-                    out=wv_codes[m][:].bitcast(FP8X4), scales=wv_sc[m][:],
-                    in_=wv_bf[:, 2 * m * HALF : 2 * (m + 1) * HALF],
+                    out=wv_codes[:, c0:c1].bitcast(FP8X4), scales=wv_sc[:, c0:c1], in_=wv_bf[:, 4 * c0 : 4 * c1]
                 )
 
-        def embed(j0, b, diff):
+        def embed(j0, width, b, diff):
             h, j = divmod(j0, HALF)
-            bank = psum.tile([P, HALF], F32, name="bank")
-            for t in range(4):
+            slots = BANK // width
+            for t0 in range(0, 4, slots):
+                bank = psum.tile([P, BANK], F32, name="bank")
                 for a in range(2):
-                    codes, scale = w8_operand(a, 4 * b + t)
-                    nc.tensor.matmul_mx(
-                        out=bank[:, t * CHUNK : (t + 1) * CHUNK], lhsT=codes, lhsT_scale=scale,
-                        rhs=v1[a][:, j0 : j0 + CHUNK].bitcast(FP8X4),
-                        rhs_scale=planes1[:].bitcast(U8)[4 * a : P, j0 : j0 + CHUNK],
-                        start=(a == 0), stop=(a == 1),
-                    )
-            nc.vector.tensor_tensor(
-                diff, bank[:].rearrange("p (t j) -> p t j", t=4), neg_b[h][b][:, :, j : j + CHUNK], ADD
-            )
+                    for t in range(slots):
+                        codes, scale = w8_operand(a, 4 * b + t0 + t)
+                        nc.tensor.matmul_mx(
+                            out=bank[:, t * width : (t + 1) * width], lhsT=codes, lhsT_scale=scale,
+                            rhs=v1[a][:, j0 : j0 + width].bitcast(FP8X4),
+                            rhs_scale=planes1[:].bitcast(U8)[4 * a : P, j0 : j0 + width],
+                            start=(a == 0 and t == 0), stop=(a == 1 and t == slots - 1),
+                        )
+                nc.vector.tensor_tensor(
+                    diff[:, t0 : t0 + slots, :], bank[:].rearrange("p (t j) -> p t j", t=slots),
+                    neg_b[h][b][:, t0 : t0 + slots, j : j + width], ALU.add,
+                )
 
         def magnitude(h_bf, diff):
             nc.scalar.activation(
-                h_bf.rearrange("p (c i t) -> p c t i", t=4, i=4),
+                h_bf[:].rearrange("p (c i t) -> p c t i", t=4, i=4),
                 diff[:].rearrange("p t (c i) -> p c t i", i=4),
                 ACT.Abs,
             )
@@ -222,12 +231,12 @@ def tile_list_loop_closure_vetting_kernel(
         def verify(j0, width, codes, scales):
             prob = held([P, 3, width], F32, "prob%d" % j0)
             for m in range(3):
-                bank = psum.tile([P, HALF], F32, name="bank")
+                bank = psum.tile([P, BANK], F32, name="bank")
                 logits = bank[:, 0:width]
                 for b in range(2):
                     nc.tensor.matmul_mx(
-                        out=logits, lhsT=wv_codes[m][:, b * P : (b + 1) * P].bitcast(FP8X4),
-                        lhsT_scale=wv_sc[m][:, b * P : (b + 1) * P],
+                        out=logits, lhsT=wv_codes[:, b * N + m * P : b * N + (m + 1) * P].bitcast(FP8X4),
+                        lhsT_scale=wv_sc[:, b * N + m * P : b * N + (m + 1) * P],
                         rhs=codes[b][:].bitcast(FP8X4), rhs_scale=scales[b][:],
                         start=(b == 0), stop=(b == 1),
                     )
@@ -242,17 +251,13 @@ def tile_list_loop_closure_vetting_kernel(
             scales = [held([P, width], U8, "h_sc%d_%d" % (j0, b)) for b in range(2)]
             for b in range(2):
                 h_bf = held([P, 4 * width], BF16, "h_bf%d_%d" % (j0, b))
-                span = min(width, 2 * CHUNK)
-                for at in range(0, width, CHUNK):
-                    if at % span == 0:
-                        diff = ring.tile([P, 4, span], F32, name="diff")
-                    embed(j0 + at, b, diff[:, :, at % span : at % span + CHUNK])
-                    if (at + CHUNK) % span == 0:
-                        magnitude(h_bf[:, 4 * (at + CHUNK - span) : 4 * (at + CHUNK)], diff)
-                    done = done + 1
-                    for due, step in waiting:
-                        if due == done:
-                            step()
+                diff = ring.tile([P, 4, width], F32, name="diff")
+                embed(j0, width, b, diff)
+                magnitude(h_bf, diff)
+                done = done + 1
+                for due, step in waiting:
+                    if due == done:
+                        step()
                 waiting.append((done + LAG, lambda h_bf=h_bf, c=codes[b], s=scales[b]: quantize_h(h_bf, c, s)))
                 if j0 == 0 and b == 1:
                     waiting.append((done + 1, quantize_wv))

@@ -33,7 +33,7 @@ def tile_list_loop_closure_vetting_kernel(
     with ExitStack() as ctx:
         keep = ctx.enter_context(tc.tile_pool(name="keep", bufs=1))
         ring = ctx.enter_context(tc.tile_pool(name="ring", bufs=4))
-        psum = ctx.enter_context(tc.psum_pool(name="psum", bufs=8))
+        psum = ctx.enter_context(tc.psum_pool(name="psum", bufs=4))
 
         def held(shape, dtype, name, tag=None):
             return keep.tile(shape, dtype, name=name, tag=tag or name, align_bytes=64)
@@ -46,6 +46,7 @@ def tile_list_loop_closure_vetting_kernel(
         w8_raw = held([P, 2 * H], I32, "w8_raw")
         w8 = held([P, 2 * H], I32, "w8")
         planes = [held([P, 2 * S // 4], I32, "plane_pass%d" % a) for a in range(2)]
+        win1 = held([P, T // 4], I32, "win1")
         ident = held([P, P], F32, "ident")
         cols = held([P, 16], F32, "cols")
         rows = held([P, P], F32, "rows")
@@ -55,20 +56,15 @@ def tile_list_loop_closure_vetting_kernel(
         def scale_rows(scales):
             return scales.rearrange("a q c -> (a q) c").bitcast(I32)
 
+        make_identity(nc, ident[:])
         for a in range(2):
             nc.gpsimd.memset(planes[a][:], 0)
-        nc.gpsimd.memset(rows[:], 0.0)
-        for b in range(2):
-            nc.gpsimd.dma_start(
-                rows[4 * b : 4 * b + 4, :].rearrange("t (g i) -> t g i", i=8),
-                dm[512 * b : 512 * (b + 1)].rearrange("(g t i) -> t g i", t=4, i=8),
-            )
-        nc.gpsimd.dma_start(rows[8:11, :], bv.rearrange("(m p) -> m p", p=P))
-        make_identity(nc, ident[:])
         nc.gpsimd.memset(planes1[:], 0)
 
         nc.vector.memset(zero[:], 0.0)
+        nc.vector.memset(rows[:], 0.0)
         nc.vector.memset(win2[0:96, :], 0)
+        nc.vector.memset(win1[:], 0)
         nc.scalar.activation(warm[:], zero[:], ACT.Sigmoid)
 
         def load_tab2(a, tag):
@@ -90,7 +86,13 @@ def tile_list_loop_closure_vetting_kernel(
             w8_raw[:].rearrange("p (a c) -> p a c", a=2),
             w8_words.rearrange("a p c i -> p a (c i)").bitcast(I32),
         )
-        stage = held([P, 2 * S // 4], I32, "stage")
+        for b in range(2):
+            nc.sync.dma_start(
+                rows[4 * b : 4 * b + 4, :].rearrange("t (g i) -> t g i", i=8),
+                dm[512 * b : 512 * (b + 1)].rearrange("(g t i) -> t g i", t=4, i=8),
+            )
+        nc.sync.dma_start(rows[8:11, :], bv.rearrange("(m p) -> m p", p=P))
+        nc.sync.dma_start(win1[0:P:4, :], tab_scales.rearrange("a q c -> q a c").bitcast(I32))
 
         def half_of(offsets, h):
             return offsets[:, h * HALF // 16 : (h + 1) * HALF // 16]
@@ -100,27 +102,28 @@ def tile_list_loop_closure_vetting_kernel(
 
         sc2 = held([P, S], U8, "sc2")
         gather(sc2[:], win2, list2[:], U8)
-        nc.vector.tensor_copy(
-            stage[ROWS, 0:256].rearrange("p (u t g i) -> p u t g i", u=2, t=4, i=2),
-            w8_sc_raw[ROWS, :].rearrange("p (u g t i) -> p u t g i", u=2, t=4, i=2),
-        )
-        nc.vector.tensor_copy(stage[ROWS, 256:512], sc2[ROWS, :].bitcast(I32))
 
-        def move(n):
-            a, r = divmod(n, 4)
-            first = 96 + 16 * a + r
-            nc.sync.dma_start(planes[a][r:P:32, :], stage[first : first + 13 : 4, :])
+        def stage_scales(a):
+            stage = held([P, 2 * S // 4], I32, "stage%d" % a)
+            nc.vector.tensor_copy(
+                stage[ROWS, 0:256].rearrange("p (u t g i) -> p u t g i", u=2, t=4, i=2),
+                w8_sc_raw[ROWS, :].rearrange("p (u g t i) -> p u t g i", u=2, t=4, i=2),
+            )
+            nc.vector.tensor_copy(stage[ROWS, 256:512], sc2[ROWS, :].bitcast(I32))
+            return stage
 
-        for n in range(6):
-            move(n)
+        def move_scales(moves, stage):
+            for n in moves:
+                a, r = divmod(n, 4)
+                first = 96 + 16 * a + r
+                nc.sync.dma_start(planes[a][r:P:32, :], stage[first : first + 13 : 4, :])
+
+        move_scales(range(2), stage_scales(0))
+        staged = stage_scales(1)
         tab2.append(load_tab2(1, "sc2"))
-        for n in range(6, 8):
-            move(n)
-        win1 = held([P, T // 4], I32, "win1", tag="win2")
-        nc.gpsimd.memset(win1[:], 0)
-        nc.sync.dma_start(win1[0:P:4, :], tab_scales.rearrange("a q c -> q a c").bitcast(I32))
+        move_scales(range(2, 8), staged)
 
-        turned = psum.tile([P, BANK], F32, name="bank")
+        turned = psum.tile([P, BANK], F32, name="query_bank")
         nc.tensor.transpose(turned[:, 0:P], rows[:], ident[:])
         nc.scalar.copy(cols[:], turned[:, 0:16])
 
@@ -178,7 +181,7 @@ def tile_list_loop_closure_vetting_kernel(
         for h in range(2):
             gather(v1[1][:, h * HALF : (h + 1) * HALF], tab[1], half_of(list1, h), U32)
 
-        wv_raw = held([P, 8 * N], F32, "wv_raw", tag="win2")
+        wv_raw = held([P, 8 * N], F32, "wv_raw", tag="win1")
         for b in range(2):
             by_slot = wv[512 * b : 512 * (b + 1), :].rearrange("(g t i) n -> t g i n", t=4, i=8)
             for t in range(4):
@@ -190,10 +193,12 @@ def tile_list_loop_closure_vetting_kernel(
 
         def quantize_wv():
             for b in range(2):
-                nc.vector.tensor_copy(
-                    wv_bf[:, 4 * b * N : 4 * (b + 1) * N].rearrange("p (c i t) -> p c t i", t=4, i=4),
-                    wv_raw[:, 4 * b * N : 4 * (b + 1) * N].rearrange("p (t c i) -> p c t i", t=4, i=4),
-                )
+                for m in range(3):
+                    nc.gpsimd.tensor_scalar(
+                        wv_bf[:, 4 * (b * N + m * P) : 4 * (b * N + (m + 1) * P)].rearrange("p (n t) -> p n t", t=4),
+                        wv_raw[:, 4 * b * N : 4 * (b + 1) * N].rearrange("p (t n) -> p n t", t=4)[:, m * P : (m + 1) * P, :],
+                        1.0, 0.0, ALU.mult, ALU.add,
+                    )
             for c0, c1 in ((0, 256), (256, 768)):
                 nc.vector.quantize_mx(
                     out=wv_codes[:, c0:c1].bitcast(FP8X4), scales=wv_sc[:, c0:c1], in_=wv_bf[:, 4 * c0 : 4 * c1]
@@ -203,7 +208,7 @@ def tile_list_loop_closure_vetting_kernel(
             h, j = divmod(j0, HALF)
             slots = BANK // width
             for t0 in range(0, 4, slots):
-                bank = psum.tile([P, BANK], F32, name="bank")
+                bank = psum.tile([P, BANK], F32, name="query_bank")
                 for a in range(2):
                     for t in range(slots):
                         codes, scale = w8_operand(a, 4 * b + t0 + t)

@@ -24,6 +24,7 @@ ROWS = slice(96, 128)
 GROUPS = (256, 256, 256, 128, 128)
 AHEAD = 4
 LAG = 2
+WV_AT = 3
 
 
 def tile_list_loop_closure_vetting_kernel(
@@ -225,16 +226,23 @@ def tile_list_loop_closure_vetting_kernel(
 
         def magnitude(h_bf, diff):
             nc.scalar.activation(
-                h_bf[:].rearrange("p (c i t) -> p c t i", t=4, i=4),
-                diff[:].rearrange("p t (c i) -> p c t i", i=4),
+                h_bf.rearrange("p (c i t) -> p c t i", t=4, i=2),
+                diff[:].rearrange("p t (c i) -> p c t i", i=2),
                 ACT.Abs,
             )
 
-        def quantize_h(h_bf, codes, scales):
-            nc.vector.quantize_mx(out=codes[:].bitcast(FP8X4), scales=scales[:], in_=h_bf[:])
-
-        def verify(j0, width, codes, scales):
+        def verify(j0, width, h_bf):
+            last = j0 + width == S
+            codes = held([P, 2 * width], U32, "h_codes%d" % j0)
+            scales = held([P, 2 * width], U8, "h_sc%d" % j0)
+            step = width if last else 2 * width
+            for c in range(0, 2 * width, step):
+                nc.vector.quantize_mx(
+                    out=codes[:, c : c + step].bitcast(FP8X4), scales=scales[:, c : c + step],
+                    in_=h_bf[:, 4 * c : 4 * (c + step)],
+                )
             prob = held([P, 3, width], F32, "prob%d" % j0)
+            rows_out = out.rearrange("(m p) j -> p m j", p=P)[:, :, j0 : j0 + width]
             for m in range(3):
                 bank = psum.tile([P, BANK], F32, name="bank")
                 logits = bank[:, 0:width]
@@ -242,32 +250,31 @@ def tile_list_loop_closure_vetting_kernel(
                     nc.tensor.matmul_mx(
                         out=logits, lhsT=wv_codes[:, b * N + m * P : b * N + (m + 1) * P].bitcast(FP8X4),
                         lhsT_scale=wv_sc[:, b * N + m * P : b * N + (m + 1) * P],
-                        rhs=codes[b][:].bitcast(FP8X4), rhs_scale=scales[b][:],
+                        rhs=codes[:, b * width : (b + 1) * width].bitcast(FP8X4),
+                        rhs_scale=scales[:, b * width : (b + 1) * width],
                         start=(b == 0), stop=(b == 1),
                     )
                 nc.scalar.activation(prob[:, m, :], logits, ACT.Sigmoid, bias=cols[:, 8 + m : 9 + m])
-            nc.sync.dma_start(out.rearrange("(m p) j -> p m j", p=P)[:, :, j0 : j0 + width], prob[:])
+                if last:
+                    nc.sync.dma_start(rows_out[:, m, :], prob[:, m, :])
+            if not last:
+                nc.sync.dma_start(rows_out, prob[:])
 
         waiting = []
         done = 0
         j0 = 0
         for width in GROUPS:
-            codes = [held([P, width], U32, "h_codes%d_%d" % (j0, b)) for b in range(2)]
-            scales = [held([P, width], U8, "h_sc%d_%d" % (j0, b)) for b in range(2)]
+            h_bf = held([P, 8 * width], BF16, "h_bf%d" % j0)
             for b in range(2):
-                h_bf = held([P, 4 * width], BF16, "h_bf%d_%d" % (j0, b))
                 diff = ring.tile([P, 4, width], F32, name="diff")
                 embed(j0, width, b, diff)
-                magnitude(h_bf, diff)
+                magnitude(h_bf[:, 4 * b * width : 4 * (b + 1) * width], diff)
                 done = done + 1
-                for due, step in waiting:
-                    if due == done:
-                        step()
-                waiting.append((done + LAG, lambda h_bf=h_bf, c=codes[b], s=scales[b]: quantize_h(h_bf, c, s)))
-                if j0 == 0 and b == 1:
-                    waiting.append((done + 1, quantize_wv))
-            waiting.append((done + LAG, lambda j0=j0, width=width, c=codes, s=scales: verify(j0, width, c, s)))
+                if done == WV_AT:
+                    quantize_wv()
+                while waiting and done >= waiting[0][0]:
+                    verify(*waiting.pop(0)[1:])
+            waiting.append((done + LAG, j0, width, h_bf))
             j0 = j0 + width
-        for due, step in waiting:
-            if due > done:
-                step()
+        for entry in waiting:
+            verify(*entry[1:])

@@ -24,7 +24,7 @@ ROWS = slice(96, 128)
 GROUPS = (256, 256, 256, 128, 128)
 AHEAD = 4
 LAG = 2
-WV_AT = 3
+WV_AT = 5
 
 
 def tile_list_loop_closure_vetting_kernel(
@@ -33,7 +33,7 @@ def tile_list_loop_closure_vetting_kernel(
     nc = tc.nc
     with ExitStack() as ctx:
         keep = ctx.enter_context(tc.tile_pool(name="keep", bufs=1))
-        ring = ctx.enter_context(tc.tile_pool(name="ring", bufs=4))
+        ring = ctx.enter_context(tc.tile_pool(name="ring", bufs=6))
         psum = ctx.enter_context(tc.psum_pool(name="psum", bufs=4))
 
         def held(shape, dtype, name, tag=None):
@@ -226,8 +226,8 @@ def tile_list_loop_closure_vetting_kernel(
 
         def magnitude(h_bf, diff):
             nc.scalar.activation(
-                h_bf.rearrange("p (c i t) -> p c t i", t=4, i=2),
-                diff[:].rearrange("p t (c i) -> p c t i", i=2),
+                h_bf.rearrange("p (c i t) -> p c t i", t=4, i=4),
+                diff[:].rearrange("p t (c i) -> p c t i", i=4),
                 ACT.Abs,
             )
 
@@ -272,7 +272,7 @@ def tile_list_loop_closure_vetting_kernel(
                 done = done + 1
                 if done == WV_AT:
                     quantize_wv()
-                while waiting and done >= waiting[0][0]:
+                while waiting and done >= max(waiting[0][0], WV_AT):
                     verify(*waiting.pop(0)[1:])
             waiting.append((done + LAG, j0, width, h_bf))
             j0 = j0 + width

@@ -106,7 +106,7 @@ def tile_list_loop_closure_vetting_kernel(
 
         def stage_scales(a):
             stage = held([P, 2 * S // 4], I32, "stage%d" % a)
-            nc.vector.tensor_copy(
+            nc.gpsimd.tensor_copy(
                 stage[ROWS, 0:256].rearrange("p (u t g i) -> p u t g i", u=2, t=4, i=2),
                 w8_sc_raw[ROWS, :].rearrange("p (u g t i) -> p u t g i", u=2, t=4, i=2),
             )
@@ -164,10 +164,11 @@ def tile_list_loop_closure_vetting_kernel(
 
         first0, second0 = pick2(0, 0), pick2(0, 1)
         tab = [load_tab(0, "tab2_0")]
-        nc.vector.tensor_copy(
-            w8[:].rearrange("p (u t g i) -> p u t g i", u=4, t=4, i=8),
-            w8_raw[:].rearrange("p (u g t i) -> p u t g i", u=4, t=4, i=8),
-        )
+        for u in range(4):
+            nc.gpsimd.tensor_copy(
+                w8[:, u * HALF : (u + 1) * HALF].rearrange("p (t g i) -> p t g i", t=4, i=8),
+                w8_raw[:, u * HALF : (u + 1) * HALF].rearrange("p (g t i) -> p t g i", t=4, i=8),
+            )
         tab.append(load_tab(1, "w8_raw"))
         first1, second1 = pick2(1, 0), pick2(1, 1)
         sc1 = held([P, S], U8, "sc1", tag="sc2")

@@ -42,7 +42,6 @@ def tile_list_loop_closure_vetting_kernel(
         list1 = held([P, S // 16], U16, "list1")
         list2 = held([P, S // 16], U16, "list2")
         win2 = held([P, T // 4], I32, "win2")
-        planes1 = held([P, S // 4], I32, "planes1")
         w8_sc_raw = held([P, H // 4], I32, "w8_sc_raw")
         w8_raw = held([P, 2 * H], I32, "w8_raw")
         w8 = held([P, 2 * H], I32, "w8")
@@ -60,7 +59,6 @@ def tile_list_loop_closure_vetting_kernel(
         make_identity(nc, ident[:])
         for a in range(2):
             nc.gpsimd.memset(planes[a][:], 0)
-        nc.gpsimd.memset(planes1[:], 0)
 
         nc.vector.memset(zero[:], 0.0)
         nc.vector.memset(rows[:], 0.0)
@@ -163,7 +161,9 @@ def tile_list_loop_closure_vetting_kernel(
                 )
 
         first0, second0 = pick2(0, 0), pick2(0, 1)
-        tab = [load_tab(0, "tab2_0")]
+        tab = [load_tab(0, "rows")]
+        sc1 = held([P, S], U8, "sc1")
+        gather(sc1[:], win1, list1[:], U8)
         for u in range(4):
             nc.gpsimd.tensor_copy(
                 w8[:, u * HALF : (u + 1) * HALF].rearrange("p (t g i) -> p t g i", t=4, i=8),
@@ -171,11 +171,11 @@ def tile_list_loop_closure_vetting_kernel(
             )
         tab.append(load_tab(1, "w8_raw"))
         first1, second1 = pick2(1, 0), pick2(1, 1)
-        sc1 = held([P, S], U8, "sc1", tag="sc2")
-        gather(sc1[:], win1, list1[:], U8)
+        archive(0, [first0, first1], AHEAD)
+        planes1 = held([P, S // 4], I32, "planes1", tag="sc2")
+        nc.gpsimd.memset(planes1[:], 0)
         for r in range(4):
             nc.sync.dma_start(planes1[r : r + 104 : 4, :], sc1[8 * r : 8 * r + 104 : 4, :].bitcast(I32))
-        archive(0, [first0, first1], AHEAD)
         archive(1, [second0, second1], 0)
 
         v1 = [held([P, S], U32, "v1_%d" % a) for a in range(2)]
@@ -183,7 +183,7 @@ def tile_list_loop_closure_vetting_kernel(
         for h in range(2):
             gather(v1[1][:, h * HALF : (h + 1) * HALF], tab[1], half_of(list1, h), U32)
 
-        wv_raw = held([P, 8 * N], F32, "wv_raw", tag="win1")
+        wv_raw = held([P, 8 * N], F32, "wv_raw", tag="v2_00")
         for b in range(2):
             by_slot = wv[512 * b : 512 * (b + 1), :].rearrange("(g t i) n -> t g i n", t=4, i=8)
             for t in range(4):

@@ -22,7 +22,7 @@ HALF = 512
 BANK = 512
 ROWS = slice(96, 128)
 GROUPS = (256, 256, 256, 128, 128)
-AHEAD = 4
+AHEAD = 6
 LAG = 2
 WV_AT = 5
 
@@ -56,12 +56,12 @@ def tile_list_loop_closure_vetting_kernel(
         def scale_rows(scales):
             return scales.rearrange("a q c -> (a q) c").bitcast(I32)
 
+        nc.gpsimd.memset(rows[:], 0.0)
         make_identity(nc, ident[:])
         for a in range(2):
             nc.gpsimd.memset(planes[a][:], 0)
 
         nc.vector.memset(zero[:], 0.0)
-        nc.vector.memset(rows[:], 0.0)
         nc.vector.memset(win2[0:96, :], 0)
         nc.vector.memset(win1[:], 0)
         nc.scalar.activation(warm[:], zero[:], ACT.Sigmoid)
@@ -81,16 +81,16 @@ def tile_list_loop_closure_vetting_kernel(
         nc.sync.dma_start(w8_sc_raw[ROWS, :], scale_rows(w8_scales))
         nc.sync.dma_start(list1[:], offs)
         tab2 = [load_tab2(0, "tab2_0")]
-        nc.sync.dma_start(
-            w8_raw[:].rearrange("p (a c) -> p a c", a=2),
-            w8_words.rearrange("a p c i -> p a (c i)").bitcast(I32),
-        )
         for b in range(2):
             nc.sync.dma_start(
                 rows[4 * b : 4 * b + 4, :].rearrange("t (g i) -> t g i", i=8),
                 dm[512 * b : 512 * (b + 1)].rearrange("(g t i) -> t g i", t=4, i=8),
             )
         nc.sync.dma_start(rows[8:11, :], bv.rearrange("(m p) -> m p", p=P))
+        nc.sync.dma_start(
+            w8_raw[:].rearrange("p (a c) -> p a c", a=2),
+            w8_words.rearrange("a p c i -> p a (c i)").bitcast(I32),
+        )
         nc.sync.dma_start(win1[0:P:4, :], tab_scales.rearrange("a q c -> q a c").bitcast(I32))
 
         def half_of(offsets, h):
@@ -117,10 +117,10 @@ def tile_list_loop_closure_vetting_kernel(
                 first = 96 + 16 * a + r
                 nc.sync.dma_start(planes[a][r:P:32, :], stage[first : first + 13 : 4, :])
 
-        move_scales(range(2), stage_scales(0))
+        move_scales(range(4), stage_scales(0))
         staged = stage_scales(1)
         tab2.append(load_tab2(1, "sc2"))
-        move_scales(range(2, 8), staged)
+        move_scales(range(4, 8), staged)
 
         turned = psum.tile([P, BANK], F32, name="query_bank")
         nc.tensor.transpose(turned[:, 0:P], rows[:], ident[:])
@@ -132,8 +132,8 @@ def tile_list_loop_closure_vetting_kernel(
                 planes[a][:].bitcast(U8)[:, r * P : (r + 1) * P],
             )
 
-        def pick2(a, h):
-            picked = held([P, HALF], U16, "v2_%d%d" % (h, a))
+        def pick2(a, h, tag=None):
+            picked = held([P, HALF], U16, "v2_%d%d" % (h, a), tag=tag)
             gather(picked[:], tab2[a], half_of(list2, h), U16)
             return picked
 
@@ -148,7 +148,7 @@ def tile_list_loop_closure_vetting_kernel(
                     start=(a == 0), stop=(a == 1),
                 )
 
-            banks = [psum.tile([P, BANK], F32, name="bank") for r in range(ahead)]
+            banks = [psum.tile([P, BANK], F32, name="bank" if r < 4 else "query_bank") for r in range(ahead)]
             for r in range(ahead):
                 archive_pass(banks[r], 0, r)
             for r in range(8):
@@ -156,12 +156,14 @@ def tile_list_loop_closure_vetting_kernel(
                     banks.append(psum.tile([P, BANK], F32, name="bank"))
                     archive_pass(banks[r], 0, r)
                 archive_pass(banks[r], 1, r)
-                nc.scalar.activation(
-                    neg_b[h][r // 4][:, r % 4, :], banks[r][:], ACT.Identity, bias=cols[:, r : r + 1], scale=-1.0
-                )
+                emptied = neg_b[h][r // 4][:, r % 4, :]
+                if 4 <= r < ahead:
+                    nc.vector.tensor_scalar(emptied, banks[r][:], -1.0, cols[:, r : r + 1], ALU.mult, ALU.add)
+                else:
+                    nc.scalar.activation(emptied, banks[r][:], ACT.Identity, bias=cols[:, r : r + 1], scale=-1.0)
 
-        first0, second0 = pick2(0, 0), pick2(0, 1)
-        tab = [load_tab(0, "rows")]
+        first0 = pick2(0, 0)
+        tab = [load_tab(0, "stage0")]
         sc1 = held([P, S], U8, "sc1")
         gather(sc1[:], win1, list1[:], U8)
         for u in range(4):
@@ -170,7 +172,7 @@ def tile_list_loop_closure_vetting_kernel(
                 w8_raw[:, u * HALF : (u + 1) * HALF].rearrange("p (g t i) -> p t g i", t=4, i=8),
             )
         tab.append(load_tab(1, "w8_raw"))
-        first1, second1 = pick2(1, 0), pick2(1, 1)
+        first1, second0, second1 = pick2(1, 0), pick2(0, 1, "stage1"), pick2(1, 1)
         archive(0, [first0, first1], AHEAD)
         planes1 = held([P, S // 4], I32, "planes1", tag="sc2")
         nc.gpsimd.memset(planes1[:], 0)
@@ -221,8 +223,8 @@ def tile_list_loop_closure_vetting_kernel(
                             start=(a == 0 and t == 0), stop=(a == 1 and t == slots - 1),
                         )
                 nc.vector.tensor_tensor(
-                    diff[:, t0 : t0 + slots, :], bank[:].rearrange("p (t j) -> p t j", t=slots),
-                    neg_b[h][b][:, t0 : t0 + slots, j : j + width], ALU.add,
+                    diff[:, t0 : t0 + slots, :], neg_b[h][b][:, t0 : t0 + slots, j : j + width],
+                    bank[:].rearrange("p (t j) -> p t j", t=slots), ALU.add,
                 )
 
         def magnitude(h_bf, diff):

@@ -91,7 +91,7 @@ def tile_list_loop_closure_vetting_kernel(
             w8_raw[:].rearrange("p (a c) -> p a c", a=2),
             w8_words.rearrange("a p c i -> p a (c i)").bitcast(I32),
         )
-        nc.sync.dma_start(win1[0:P:4, :], tab_scales.rearrange("a q c -> q a c").bitcast(I32))
+        nc.sync.dma_start(win1[32:96:2, :], tab_scales.rearrange("a q c -> q a c").bitcast(I32))
 
         def half_of(offsets, h):
             return offsets[:, h * HALF // 16 : (h + 1) * HALF // 16]
@@ -166,6 +166,9 @@ def tile_list_loop_closure_vetting_kernel(
         tab = [load_tab(0, "stage0")]
         sc1 = held([P, S], U8, "sc1")
         gather(sc1[:], win1, list1[:], U8)
+        planes1 = held([P, S // 4], I32, "planes1")
+        for r in range(4):
+            nc.sync.dma_start(planes1[r:P:4, :], sc1[32 + 4 * r : 96 + 4 * r : 2, :].bitcast(I32))
         for u in range(4):
             nc.gpsimd.tensor_copy(
                 w8[:, u * HALF : (u + 1) * HALF].rearrange("p (t g i) -> p t g i", t=4, i=8),
@@ -174,10 +177,6 @@ def tile_list_loop_closure_vetting_kernel(
         tab.append(load_tab(1, "w8_raw"))
         first1, second0, second1 = pick2(1, 0), pick2(0, 1, "stage1"), pick2(1, 1)
         archive(0, [first0, first1], AHEAD)
-        planes1 = held([P, S // 4], I32, "planes1", tag="sc2")
-        nc.gpsimd.memset(planes1[:], 0)
-        for r in range(4):
-            nc.sync.dma_start(planes1[r : r + 104 : 4, :], sc1[8 * r : 8 * r + 104 : 4, :].bitcast(I32))
         archive(1, [second0, second1], 0)
 
         v1 = [held([P, S], U32, "v1_%d" % a) for a in range(2)]

@@ -1,7 +1,6 @@
 from contextlib import ExitStack
 
 import concourse.mybir as mybir
-from concourse.masks import make_identity
 
 K, T, S, H, N = 1024, 4096, 1024, 1024, 384
 FLOPS = 2 * 2 * K * H * S + 2 * H * N * S
@@ -22,7 +21,7 @@ HALF = 512
 BANK = 512
 ROWS = slice(96, 128)
 GROUPS = (256, 256, 256, 128, 128)
-AHEAD = 6
+AHEAD = 8
 LAG = 2
 WV_AT = 5
 
@@ -42,25 +41,20 @@ def tile_list_loop_closure_vetting_kernel(
         list1 = held([P, S // 16], U16, "list1")
         list2 = held([P, S // 16], U16, "list2")
         win2 = held([P, T // 4], I32, "win2")
+        win1 = held([P, T // 4], I32, "win1")
         w8_sc_raw = held([P, H // 4], I32, "w8_sc_raw")
         w8_raw = held([P, 2 * H], I32, "w8_raw")
-        w8 = held([P, 2 * H], I32, "w8")
-        planes = [held([P, 2 * S // 4], I32, "plane_pass%d" % a) for a in range(2)]
-        win1 = held([P, T // 4], I32, "win1")
-        ident = held([P, P], F32, "ident")
-        cols = held([P, 16], F32, "cols")
-        rows = held([P, P], F32, "rows")
+        w8 = held([P, 2 * H], U32, "w8")
+        planes = [held([P, 2 * S // 4], I32, "plane_pass0")]
+        dm_cols = held([P, 8], F32, "dm_cols")
         warm = held([P, 1], F32, "warm")
         zero = held([P, 1], F32, "zero")
 
         def scale_rows(scales):
             return scales.rearrange("a q c -> (a q) c").bitcast(I32)
 
-        nc.gpsimd.memset(rows[:], 0.0)
-        make_identity(nc, ident[:])
-        for a in range(2):
-            nc.gpsimd.memset(planes[a][:], 0)
-
+        nc.gpsimd.memset(w8_sc_raw[0:96, :], 0)
+        nc.gpsimd.memset(planes[0][:], 0)
         nc.vector.memset(zero[:], 0.0)
         nc.vector.memset(win2[0:96, :], 0)
         nc.vector.memset(win1[:], 0)
@@ -79,22 +73,19 @@ def tile_list_loop_closure_vetting_kernel(
         nc.sync.dma_start(list2[:], offs2)
         nc.sync.dma_start(win2[ROWS, :], scale_rows(tab2_scales))
         nc.sync.dma_start(w8_sc_raw[ROWS, :], scale_rows(w8_scales))
-        nc.sync.dma_start(list1[:], offs)
         tab2 = [load_tab2(0, "tab2_0")]
-        for b in range(2):
-            nc.sync.dma_start(
-                rows[4 * b : 4 * b + 4, :].rearrange("t (g i) -> t g i", i=8),
-                dm[512 * b : 512 * (b + 1)].rearrange("(g t i) -> t g i", t=4, i=8),
-            )
-        nc.sync.dma_start(rows[8:11, :], bv.rearrange("(m p) -> m p", p=P))
+        nc.sync.dma_start(list1[:], offs)
+        nc.sync.dma_start(
+            dm_cols[:].rearrange("p (b t) -> p b t", t=4), dm.rearrange("(b p t) -> p b t", b=2, t=4)
+        )
         nc.sync.dma_start(
             w8_raw[:].rearrange("p (a c) -> p a c", a=2),
             w8_words.rearrange("a p c i -> p a (c i)").bitcast(I32),
         )
         nc.sync.dma_start(win1[32:96:2, :], tab_scales.rearrange("a q c -> q a c").bitcast(I32))
 
-        def half_of(offsets, h):
-            return offsets[:, h * HALF // 16 : (h + 1) * HALF // 16]
+        def part_of(offsets, j0, width):
+            return offsets[:, j0 // 16 : (j0 + width) // 16]
 
         def gather(picked, window, offsets, dtype):
             nc.vector.tensor_copy(picked, window[:].bitcast(dtype).indirect(offsets))
@@ -102,29 +93,31 @@ def tile_list_loop_closure_vetting_kernel(
         sc2 = held([P, S], U8, "sc2")
         gather(sc2[:], win2, list2[:], U8)
 
-        def stage_scales(a):
-            stage = held([P, 2 * S // 4], I32, "stage%d" % a)
-            nc.gpsimd.tensor_copy(
-                stage[ROWS, 0:256].rearrange("p (u t g i) -> p u t g i", u=2, t=4, i=2),
-                w8_sc_raw[ROWS, :].rearrange("p (u g t i) -> p u t g i", u=2, t=4, i=2),
-            )
-            nc.vector.tensor_copy(stage[ROWS, 256:512], sc2[ROWS, :].bitcast(I32))
-            return stage
+        stage = held([P, 2 * S // 4], I32, "stage")
+        nc.gpsimd.tensor_copy(
+            stage[:].bitcast(U8)[:, 0:H].rearrange("p (b t m) -> p b t m", b=2, t=4),
+            w8_sc_raw[:].bitcast(U8).rearrange("p (b m t) -> p b t m", b=2, t=4),
+        )
+        nc.vector.tensor_copy(stage[ROWS, 256:512], sc2[ROWS, :].bitcast(I32))
 
-        def move_scales(moves, stage):
-            for n in moves:
-                a, r = divmod(n, 4)
+        def move_scales(a):
+            for r in range(4):
                 first = 96 + 16 * a + r
                 nc.sync.dma_start(planes[a][r:P:32, :], stage[first : first + 13 : 4, :])
 
-        move_scales(range(4), stage_scales(0))
-        staged = stage_scales(1)
+        move_scales(0)
         tab2.append(load_tab2(1, "sc2"))
-        move_scales(range(4, 8), staged)
+        planes.append(held([P, 2 * S // 4], I32, "plane_pass1", tag="win2"))
+        nc.gpsimd.memset(planes[1][:], 0)
+        move_scales(1)
 
-        turned = psum.tile([P, BANK], F32, name="query_bank")
-        nc.tensor.transpose(turned[:, 0:P], rows[:], ident[:])
-        nc.scalar.copy(cols[:], turned[:, 0:16])
+        for a in range(2):
+            for b in range(2):
+                cols = slice(a * H + b * HALF, a * H + (b + 1) * HALF)
+                nc.scalar.copy(
+                    w8[:, cols].rearrange("p (t m) -> p m t", t=4),
+                    w8_raw[:, cols].bitcast(U32).rearrange("p (m t) -> p m t", t=4),
+                )
 
         def w8_operand(a, r):
             return (
@@ -134,7 +127,7 @@ def tile_list_loop_closure_vetting_kernel(
 
         def pick2(a, h, tag=None):
             picked = held([P, HALF], U16, "v2_%d%d" % (h, a), tag=tag)
-            gather(picked[:], tab2[a], half_of(list2, h), U16)
+            gather(picked[:], tab2[a], part_of(list2, h * HALF, HALF), U16)
             return picked
 
         neg_b = [[held([P, 4, HALF], F32, "neg_b%d%d" % (h, b)) for b in range(2)] for h in range(2)]
@@ -158,37 +151,37 @@ def tile_list_loop_closure_vetting_kernel(
                 archive_pass(banks[r], 1, r)
                 emptied = neg_b[h][r // 4][:, r % 4, :]
                 if 4 <= r < ahead:
-                    nc.vector.tensor_scalar(emptied, banks[r][:], -1.0, cols[:, r : r + 1], ALU.mult, ALU.add)
+                    nc.vector.tensor_scalar(emptied, banks[r][:], -1.0, dm_cols[:, r : r + 1], ALU.mult, ALU.add)
                 else:
-                    nc.scalar.activation(emptied, banks[r][:], ACT.Identity, bias=cols[:, r : r + 1], scale=-1.0)
+                    nc.scalar.activation(emptied, banks[r][:], ACT.Identity, bias=dm_cols[:, r : r + 1], scale=-1.0)
 
-        first0 = pick2(0, 0)
-        tab = [load_tab(0, "stage0")]
+        first0, second0 = pick2(0, 0), pick2(0, 1)
+        tab = [load_tab(0, "tab2_0")]
         sc1 = held([P, S], U8, "sc1")
         gather(sc1[:], win1, list1[:], U8)
         planes1 = held([P, S // 4], I32, "planes1")
         for r in range(4):
             nc.sync.dma_start(planes1[r:P:4, :], sc1[32 + 4 * r : 96 + 4 * r : 2, :].bitcast(I32))
-        for u in range(4):
-            nc.gpsimd.tensor_copy(
-                w8[:, u * HALF : (u + 1) * HALF].rearrange("p (t g i) -> p t g i", t=4, i=8),
-                w8_raw[:, u * HALF : (u + 1) * HALF].rearrange("p (g t i) -> p t g i", t=4, i=8),
-            )
-        tab.append(load_tab(1, "w8_raw"))
-        first1, second0, second1 = pick2(1, 0), pick2(0, 1, "stage1"), pick2(1, 1)
+        tab.append(load_tab(1, "win1"))
+        first1, second1 = pick2(1, 0), pick2(1, 1)
         archive(0, [first0, first1], AHEAD)
         archive(1, [second0, second1], 0)
 
         v1 = [held([P, S], U32, "v1_%d" % a) for a in range(2)]
-        gather(v1[0][:], tab[0], list1[:], U32)
-        for h in range(2):
-            gather(v1[1][:, h * HALF : (h + 1) * HALF], tab[1], half_of(list1, h), U32)
 
-        wv_raw = held([P, 8 * N], F32, "wv_raw", tag="v2_00")
+        def pick1(a, j0, width):
+            gather(v1[a][:, j0 : j0 + width], tab[a], part_of(list1, j0, width), U32)
+
+        pick1(0, 0, S)
+        pick1(1, 0, 256)
+        pick1(1, 256, 256)
+
+        wv_raw = [held([P, 4 * N], F32, "wv_raw%d" % b, tag="v2_0%d" % b) for b in range(2)]
         for b in range(2):
-            by_slot = wv[512 * b : 512 * (b + 1), :].rearrange("(g t i) n -> t g i n", t=4, i=8)
-            for t in range(4):
-                nc.sync.dma_start(wv_raw[:, (4 * b + t) * N : (4 * b + t + 1) * N], by_slot[t])
+            nc.sync.dma_start(wv_raw[b][:], wv[512 * b : 512 * (b + 1), :].rearrange("(p t) n -> p (t n)", t=4))
+        bv_cols = held([P, 3], F32, "bv_cols", tag="v2_10")
+        with nc.allow_non_contiguous_dma(reason="one bias value a partition"):
+            nc.sync.dma_start(bv_cols[:], bv.rearrange("(m p) -> p m", p=P))
 
         wv_codes = held([P, 2 * N], U32, "wv_codes")
         wv_sc = held([P, 2 * N], U8, "wv_sc")
@@ -199,7 +192,7 @@ def tile_list_loop_closure_vetting_kernel(
                 for m in range(3):
                     nc.gpsimd.tensor_scalar(
                         wv_bf[:, 4 * (b * N + m * P) : 4 * (b * N + (m + 1) * P)].rearrange("p (n t) -> p n t", t=4),
-                        wv_raw[:, 4 * b * N : 4 * (b + 1) * N].rearrange("p (t n) -> p n t", t=4)[:, m * P : (m + 1) * P, :],
+                        wv_raw[b][:].rearrange("p (t n) -> p n t", t=4)[:, m * P : (m + 1) * P, :],
                         1.0, 0.0, ALU.mult, ALU.add,
                     )
             for c0, c1 in ((0, 256), (256, 768)):
@@ -256,7 +249,7 @@ def tile_list_loop_closure_vetting_kernel(
                         rhs_scale=scales[:, b * width : (b + 1) * width],
                         start=(b == 0), stop=(b == 1),
                     )
-                nc.scalar.activation(prob[:, m, :], logits, ACT.Sigmoid, bias=cols[:, 8 + m : 9 + m])
+                nc.scalar.activation(prob[:, m, :], logits, ACT.Sigmoid, bias=bv_cols[:, m : m + 1])
                 if last:
                     nc.sync.dma_start(rows_out[:, m, :], prob[:, m, :])
             if not last:
@@ -268,10 +261,14 @@ def tile_list_loop_closure_vetting_kernel(
         for width in GROUPS:
             h_bf = held([P, 8 * width], BF16, "h_bf%d" % j0)
             for b in range(2):
-                diff = ring.tile([P, 4, width], F32, name="diff")
-                embed(j0, width, b, diff)
-                magnitude(h_bf[:, 4 * b * width : 4 * (b + 1) * width], diff)
+                piece = P if done == 0 else width
+                for c in range(0, width, piece):
+                    diff = ring.tile([P, 4, piece], F32, name="diff")
+                    embed(j0 + c, piece, b, diff)
+                    magnitude(h_bf[:, 4 * (b * width + c) : 4 * (b * width + c + piece)], diff)
                 done = done + 1
+                if done == 2:
+                    pick1(1, HALF, HALF)
                 if done == WV_AT:
                     quantize_wv()
                 while waiting and done >= max(waiting[0][0], WV_AT):

@@ -19,11 +19,10 @@ ALU = mybir.AluOpType
 P = 128
 HALF = 512
 BANK = 512
+QUARTER = 256
 ROWS = slice(96, 128)
 GROUPS = (256, 256, 256, 128, 128)
 AHEAD = 8
-LAG = 2
-WV_AT = 5
 
 
 def tile_list_loop_closure_vetting_kernel(
@@ -167,14 +166,24 @@ def tile_list_loop_closure_vetting_kernel(
         archive(0, [first0, first1], AHEAD)
         archive(1, [second0, second1], 0)
 
-        v1 = [held([P, S], U32, "v1_%d" % a) for a in range(2)]
+        v1_first = held([P, S], U32, "v1_first")
+        gather(v1_first[:], tab[0], list1[:], U32)
+        v1_second = []
 
-        def pick1(a, j0, width):
-            gather(v1[a][:, j0 : j0 + width], tab[a], part_of(list1, j0, width), U32)
+        def pick_quarter(tag=None):
+            q = len(v1_second)
+            picked = held([P, QUARTER], U32, "v1_second%d" % q, tag=tag)
+            gather(picked[:], tab[1], part_of(list1, q * QUARTER, QUARTER), U32)
+            v1_second.append(picked)
 
-        pick1(0, 0, S)
-        pick1(1, 0, 256)
-        pick1(1, 256, 256)
+        def v1(a, j0, width):
+            if a == 0:
+                return v1_first[:, j0 : j0 + width]
+            q, j = divmod(j0, QUARTER)
+            return v1_second[q][:, j : j + width]
+
+        pick_quarter()
+        pick_quarter()
 
         wv_raw = [held([P, 4 * N], F32, "wv_raw%d" % b, tag="v2_0%d" % b) for b in range(2)]
         for b in range(2):
@@ -185,22 +194,33 @@ def tile_list_loop_closure_vetting_kernel(
 
         wv_codes = held([P, 2 * N], U32, "wv_codes")
         wv_sc = held([P, 2 * N], U8, "wv_sc")
-        wv_bf = held([P, 6 * HALF], BF16, "wv_bf")
+        wv_bf = held([P, 8 * N], BF16, "wv_bf")
 
-        def quantize_wv():
+        def wv_cols(m, b):
+            return slice((2 * m + b) * P, (2 * m + b + 1) * P)
+
+        def round_wv():
             for b in range(2):
-                for m in range(3):
+                for m in (2, 1, 0):
+                    cols = wv_cols(m, b)
                     nc.gpsimd.tensor_scalar(
-                        wv_bf[:, 4 * (b * N + m * P) : 4 * (b * N + (m + 1) * P)].rearrange("p (n t) -> p n t", t=4),
+                        wv_bf[:, 4 * cols.start : 4 * cols.stop].rearrange("p (n t) -> p n t", t=4),
                         wv_raw[b][:].rearrange("p (t n) -> p n t", t=4)[:, m * P : (m + 1) * P, :],
                         1.0, 0.0, ALU.mult, ALU.add,
                     )
-            for c0, c1 in ((0, 256), (256, 768)):
-                nc.vector.quantize_mx(
-                    out=wv_codes[:, c0:c1].bitcast(FP8X4), scales=wv_sc[:, c0:c1], in_=wv_bf[:, 4 * c0 : 4 * c1]
-                )
 
-        def embed(j0, width, b, diff):
+        def quantize_wv(c0, c1):
+            nc.vector.quantize_mx(
+                out=wv_codes[:, c0:c1].bitcast(FP8X4), scales=wv_sc[:, c0:c1], in_=wv_bf[:, 4 * c0 : 4 * c1]
+            )
+
+        starts = [sum(GROUPS[:g]) for g in range(len(GROUPS))]
+        h_bf = [held([P, 8 * width], BF16, "h_bf%d" % g) for g, width in enumerate(GROUPS)]
+        h_codes = [held([P, 2 * width], U32, "h_codes%d" % g) for g, width in enumerate(GROUPS)]
+        h_sc = [held([P, 2 * width], U8, "h_sc%d" % g) for g, width in enumerate(GROUPS)]
+        prob = [held([P, 3, width], F32, "prob%d" % g) for g, width in enumerate(GROUPS)]
+
+        def embed(j0, width, b, diff, woven):
             h, j = divmod(j0, HALF)
             slots = BANK // width
             for t0 in range(0, 4, slots):
@@ -210,70 +230,111 @@ def tile_list_loop_closure_vetting_kernel(
                         codes, scale = w8_operand(a, 4 * b + t0 + t)
                         nc.tensor.matmul_mx(
                             out=bank[:, t * width : (t + 1) * width], lhsT=codes, lhsT_scale=scale,
-                            rhs=v1[a][:, j0 : j0 + width].bitcast(FP8X4),
+                            rhs=v1(a, j0, width).bitcast(FP8X4),
                             rhs_scale=planes1[:].bitcast(U8)[4 * a : P, j0 : j0 + width],
                             start=(a == 0 and t == 0), stop=(a == 1 and t == slots - 1),
                         )
-                nc.vector.tensor_tensor(
-                    diff[:, t0 : t0 + slots, :], neg_b[h][b][:, t0 : t0 + slots, j : j + width],
-                    bank[:].rearrange("p (t j) -> p t j", t=slots), ALU.add,
+                if woven:
+                    nc.vector.tensor_tensor(
+                        diff[:].rearrange("p t j -> p (t j)").rearrange("p (c i t) -> p c t i", t=4, i=4),
+                        neg_b[h][b][:, :, j : j + width].rearrange("p t (c i) -> p c t i", i=4),
+                        bank[:].rearrange("p (t c i) -> p c t i", t=4, i=4), ALU.add,
+                    )
+                else:
+                    nc.vector.tensor_tensor(
+                        diff[:, t0 : t0 + slots, :], neg_b[h][b][:, t0 : t0 + slots, j : j + width],
+                        bank[:].rearrange("p (t j) -> p t j", t=slots), ALU.add,
+                    )
+
+        def unit(g, b, piece=None, tag=None):
+            width = GROUPS[g]
+            piece = piece or width
+            for c in range(0, width, piece):
+                diff = held([P, 4, piece], F32, tag) if tag else ring.tile([P, 4, piece], F32, name="diff")
+                embed(starts[g] + c, piece, b, diff, False)
+                nc.scalar.activation(
+                    h_bf[g][:, 4 * (b * width + c) : 4 * (b * width + c + piece)].rearrange(
+                        "p (c i t) -> p c t i", t=4, i=4
+                    ),
+                    diff[:].rearrange("p t (c i) -> p c t i", i=4),
+                    ACT.Abs,
                 )
 
-        def magnitude(h_bf, diff):
-            nc.scalar.activation(
-                h_bf.rearrange("p (c i t) -> p c t i", t=4, i=4),
-                diff[:].rearrange("p t (c i) -> p c t i", i=4),
-                ACT.Abs,
+        def woven_difference(g, b):
+            diff = ring.tile([P, 4, P], F32, name="diff")
+            embed(starts[g], P, b, diff, True)
+            return diff[:].rearrange("p t j -> p (t j)")
+
+        def vector_magnitude(g, b, flat):
+            nc.vector.scalar_tensor_tensor(h_bf[g][:, 4 * b * P : 4 * (b + 1) * P], flat, -1.0, flat, ALU.mult, ALU.max)
+
+        def quantize_h(g, c0=0, c1=None):
+            c1 = c1 or 2 * GROUPS[g]
+            nc.vector.quantize_mx(
+                out=h_codes[g][:, c0:c1].bitcast(FP8X4), scales=h_sc[g][:, c0:c1], in_=h_bf[g][:, 4 * c0 : 4 * c1]
             )
 
-        def verify(j0, width, h_bf):
-            last = j0 + width == S
-            codes = held([P, 2 * width], U32, "h_codes%d" % j0)
-            scales = held([P, 2 * width], U8, "h_sc%d" % j0)
-            step = width if last else 2 * width
-            for c in range(0, 2 * width, step):
-                nc.vector.quantize_mx(
-                    out=codes[:, c : c + step].bitcast(FP8X4), scales=scales[:, c : c + step],
-                    in_=h_bf[:, 4 * c : 4 * (c + step)],
-                )
-            prob = held([P, 3, width], F32, "prob%d" % j0)
-            rows_out = out.rearrange("(m p) j -> p m j", p=P)[:, :, j0 : j0 + width]
-            for m in range(3):
-                bank = psum.tile([P, BANK], F32, name="bank")
-                logits = bank[:, 0:width]
-                for b in range(2):
-                    nc.tensor.matmul_mx(
-                        out=logits, lhsT=wv_codes[:, b * N + m * P : b * N + (m + 1) * P].bitcast(FP8X4),
-                        lhsT_scale=wv_sc[:, b * N + m * P : b * N + (m + 1) * P],
-                        rhs=codes[:, b * width : (b + 1) * width].bitcast(FP8X4),
-                        rhs_scale=scales[:, b * width : (b + 1) * width],
-                        start=(b == 0), stop=(b == 1),
-                    )
-                nc.scalar.activation(prob[:, m, :], logits, ACT.Sigmoid, bias=bv_cols[:, m : m + 1])
-                if last:
-                    nc.sync.dma_start(rows_out[:, m, :], prob[:, m, :])
-            if not last:
-                nc.sync.dma_start(rows_out, prob[:])
+        def logits_pass(logits, g, m, b):
+            width = GROUPS[g]
+            nc.tensor.matmul_mx(
+                out=logits, lhsT=wv_codes[:, wv_cols(m, b)].bitcast(FP8X4), lhsT_scale=wv_sc[:, wv_cols(m, b)],
+                rhs=h_codes[g][:, b * width : (b + 1) * width].bitcast(FP8X4),
+                rhs_scale=h_sc[g][:, b * width : (b + 1) * width],
+                start=(b == 0), stop=(b == 1),
+            )
 
-        waiting = []
-        done = 0
-        j0 = 0
-        for width in GROUPS:
-            h_bf = held([P, 8 * width], BF16, "h_bf%d" % j0)
+        def rows_out(g):
+            return out.rearrange("(m p) j -> p m j", p=P)[:, :, starts[g] : starts[g] + GROUPS[g]]
+
+        def sigmoid(logits, g, m):
+            nc.scalar.activation(prob[g][:, m, :], logits, ACT.Sigmoid, bias=bv_cols[:, m : m + 1])
+
+        def verify(g, tiles):
+            width = GROUPS[g]
+            bank = psum.tile([P, BANK], F32, name="bank")
+            for n, m in enumerate(tiles):
+                for b in range(2):
+                    logits_pass(bank[:, n * width : (n + 1) * width], g, m, b)
+            for n, m in enumerate(tiles):
+                sigmoid(bank[:, n * width : (n + 1) * width], g, m)
+            if 2 in tiles:
+                nc.sync.dma_start(rows_out(g), prob[g][:])
+
+        def verify_last(g):
+            banks = [psum.tile([P, BANK], F32, name="query_bank") for m in range(3)]
             for b in range(2):
-                piece = P if done == 0 else width
-                for c in range(0, width, piece):
-                    diff = ring.tile([P, 4, piece], F32, name="diff")
-                    embed(j0 + c, piece, b, diff)
-                    magnitude(h_bf[:, 4 * (b * width + c) : 4 * (b * width + c + piece)], diff)
-                done = done + 1
-                if done == 2:
-                    pick1(1, HALF, HALF)
-                if done == WV_AT:
-                    quantize_wv()
-                while waiting and done >= max(waiting[0][0], WV_AT):
-                    verify(*waiting.pop(0)[1:])
-            waiting.append((done + LAG, j0, width, h_bf))
-            j0 = j0 + width
-        for entry in waiting:
-            verify(*entry[1:])
+                quantize_h(g, b * P, (b + 1) * P)
+                for m in range(3):
+                    logits_pass(banks[m][:, 0:P], g, m, b)
+            for m in range(3):
+                sigmoid(banks[m][:, 0:P], g, m)
+                nc.sync.dma_start(rows_out(g)[:, m, :], prob[g][:, m, :])
+
+        round_wv()
+        unit(0, 0, tag="diff_first")
+        unit(0, 1, tag="diff_second")
+        pick_quarter("diff_first")
+        unit(1, 0)
+        unit(1, 1)
+        quantize_wv(0, 256)
+        quantize_h(0)
+        verify(0, [0])
+        quantize_wv(256, 768)
+        verify(0, [1, 2])
+        pick_quarter("diff_second")
+        unit(2, 0)
+        unit(2, 1)
+        quantize_h(1)
+        verify(1, [0])
+        verify(1, [1, 2])
+        unit(3, 0)
+        unit(3, 1)
+        quantize_h(2)
+        verify(2, [0])
+        verify(2, [1, 2])
+        unit(4, 0)
+        flat = woven_difference(4, 1)
+        quantize_h(3)
+        vector_magnitude(4, 1, flat)
+        verify(3, [0, 1, 2])
+        verify_last(4)

@@ -201,13 +201,11 @@ def tile_list_loop_closure_vetting_kernel(
 
         def round_wv():
             for b in range(2):
-                for m in (2, 1, 0):
-                    cols = wv_cols(m, b)
-                    nc.gpsimd.tensor_scalar(
-                        wv_bf[:, 4 * cols.start : 4 * cols.stop].rearrange("p (n t) -> p n t", t=4),
-                        wv_raw[b][:].rearrange("p (t n) -> p n t", t=4)[:, m * P : (m + 1) * P, :],
-                        1.0, 0.0, ALU.mult, ALU.add,
-                    )
+                nc.gpsimd.tensor_scalar(
+                    wv_bf[:].rearrange("p (m b n t) -> p b m n t", b=2, n=P, t=4)[:, b],
+                    wv_raw[b][:].rearrange("p (t m n) -> p m n t", t=4, n=P),
+                    1.0, 0.0, ALU.mult, ALU.add,
+                )
 
         def quantize_wv(c0, c1):
             nc.vector.quantize_mx(
@@ -220,7 +218,7 @@ def tile_list_loop_closure_vetting_kernel(
         h_sc = [held([P, 2 * width], U8, "h_sc%d" % g) for g, width in enumerate(GROUPS)]
         prob = [held([P, 3, width], F32, "prob%d" % g) for g, width in enumerate(GROUPS)]
 
-        def embed(j0, width, b, diff, woven):
+        def embed(j0, width, b, diff):
             h, j = divmod(j0, HALF)
             slots = BANK // width
             for t0 in range(0, 4, slots):
@@ -234,24 +232,17 @@ def tile_list_loop_closure_vetting_kernel(
                             rhs_scale=planes1[:].bitcast(U8)[4 * a : P, j0 : j0 + width],
                             start=(a == 0 and t == 0), stop=(a == 1 and t == slots - 1),
                         )
-                if woven:
-                    nc.vector.tensor_tensor(
-                        diff[:].rearrange("p t j -> p (t j)").rearrange("p (c i t) -> p c t i", t=4, i=4),
-                        neg_b[h][b][:, :, j : j + width].rearrange("p t (c i) -> p c t i", i=4),
-                        bank[:].rearrange("p (t c i) -> p c t i", t=4, i=4), ALU.add,
-                    )
-                else:
-                    nc.vector.tensor_tensor(
-                        diff[:, t0 : t0 + slots, :], neg_b[h][b][:, t0 : t0 + slots, j : j + width],
-                        bank[:].rearrange("p (t j) -> p t j", t=slots), ALU.add,
-                    )
+                nc.vector.tensor_tensor(
+                    diff[:, t0 : t0 + slots, :], neg_b[h][b][:, t0 : t0 + slots, j : j + width],
+                    bank[:].rearrange("p (t j) -> p t j", t=slots), ALU.add,
+                )
 
         def unit(g, b, piece=None, tag=None):
             width = GROUPS[g]
             piece = piece or width
             for c in range(0, width, piece):
                 diff = held([P, 4, piece], F32, tag) if tag else ring.tile([P, 4, piece], F32, name="diff")
-                embed(starts[g] + c, piece, b, diff, False)
+                embed(starts[g] + c, piece, b, diff)
                 nc.scalar.activation(
                     h_bf[g][:, 4 * (b * width + c) : 4 * (b * width + c + piece)].rearrange(
                         "p (c i t) -> p c t i", t=4, i=4
@@ -259,14 +250,6 @@ def tile_list_loop_closure_vetting_kernel(
                     diff[:].rearrange("p t (c i) -> p c t i", i=4),
                     ACT.Abs,
                 )
-
-        def woven_difference(g, b):
-            diff = ring.tile([P, 4, P], F32, name="diff")
-            embed(starts[g], P, b, diff, True)
-            return diff[:].rearrange("p t j -> p (t j)")
-
-        def vector_magnitude(g, b, flat):
-            nc.vector.scalar_tensor_tensor(h_bf[g][:, 4 * b * P : 4 * (b + 1) * P], flat, -1.0, flat, ALU.mult, ALU.max)
 
         def quantize_h(g, c0=0, c1=None):
             c1 = c1 or 2 * GROUPS[g]
@@ -333,8 +316,7 @@ def tile_list_loop_closure_vetting_kernel(
         verify(2, [0])
         verify(2, [1, 2])
         unit(4, 0)
-        flat = woven_difference(4, 1)
+        unit(4, 1)
         quantize_h(3)
-        vector_magnitude(4, 1, flat)
         verify(3, [0, 1, 2])
         verify_last(4)

@@ -158,10 +158,10 @@ def tile_list_loop_closure_vetting_kernel(
         tab = [load_tab(0, "tab2_0")]
         sc1 = held([P, S], U8, "sc1")
         gather(sc1[:], win1, list1[:], U8)
-        planes1 = held([P, S // 4], I32, "planes1")
+        tab.append(load_tab(1, "win1"))
+        planes1 = held([P, S // 4], I32, "planes1", tag="w8_raw")
         for r in range(4):
             nc.sync.dma_start(planes1[r:P:4, :], sc1[32 + 4 * r : 96 + 4 * r : 2, :].bitcast(I32))
-        tab.append(load_tab(1, "win1"))
         first1, second1 = pick2(1, 0), pick2(1, 1)
         archive(0, [first0, first1], AHEAD)
         archive(1, [second0, second1], 0)
@@ -218,38 +218,50 @@ def tile_list_loop_closure_vetting_kernel(
         h_sc = [held([P, 2 * width], U8, "h_sc%d" % g) for g, width in enumerate(GROUPS)]
         prob = [held([P, 3, width], F32, "prob%d" % g) for g, width in enumerate(GROUPS)]
 
-        def embed(j0, width, b, diff):
-            h, j = divmod(j0, HALF)
+        def query_bank(j0, width, b, t0):
             slots = BANK // width
+            bank = psum.tile([P, BANK], F32, name="query_bank")
+            for a in range(2):
+                for t in range(slots):
+                    codes, scale = w8_operand(a, 4 * b + t0 + t)
+                    nc.tensor.matmul_mx(
+                        out=bank[:, t * width : (t + 1) * width], lhsT=codes, lhsT_scale=scale,
+                        rhs=v1(a, j0, width).bitcast(FP8X4),
+                        rhs_scale=planes1[:].bitcast(U8)[4 * a : P, j0 : j0 + width],
+                        start=(a == 0 and t == 0), stop=(a == 1 and t == slots - 1),
+                    )
+            return bank
+
+        def magnitude(g, first, diff):
+            nc.scalar.activation(
+                h_bf[g][:, 4 * first : 4 * (first + diff.shape[2])].rearrange("p (c i t) -> p c t i", t=4, i=4),
+                diff[:].rearrange("p t (c i) -> p c t i", i=4),
+                ACT.Abs,
+            )
+
+        def unit(g, b, tag=None):
+            width = GROUPS[g]
+            slots = BANK // width
+            h, j = divmod(starts[g], HALF)
+            diff = held([P, 4, width], F32, tag) if tag else ring.tile([P, 4, width], F32, name="diff")
             for t0 in range(0, 4, slots):
-                bank = psum.tile([P, BANK], F32, name="query_bank")
-                for a in range(2):
-                    for t in range(slots):
-                        codes, scale = w8_operand(a, 4 * b + t0 + t)
-                        nc.tensor.matmul_mx(
-                            out=bank[:, t * width : (t + 1) * width], lhsT=codes, lhsT_scale=scale,
-                            rhs=v1(a, j0, width).bitcast(FP8X4),
-                            rhs_scale=planes1[:].bitcast(U8)[4 * a : P, j0 : j0 + width],
-                            start=(a == 0 and t == 0), stop=(a == 1 and t == slots - 1),
-                        )
+                bank = query_bank(starts[g], width, b, t0)
                 nc.vector.tensor_tensor(
                     diff[:, t0 : t0 + slots, :], neg_b[h][b][:, t0 : t0 + slots, j : j + width],
                     bank[:].rearrange("p (t j) -> p t j", t=slots), ALU.add,
                 )
+            magnitude(g, b * width, diff)
 
-        def unit(g, b, piece=None, tag=None):
-            width = GROUPS[g]
-            piece = piece or width
-            for c in range(0, width, piece):
-                diff = held([P, 4, piece], F32, tag) if tag else ring.tile([P, 4, piece], F32, name="diff")
-                embed(starts[g] + c, piece, b, diff)
-                nc.scalar.activation(
-                    h_bf[g][:, 4 * (b * width + c) : 4 * (b * width + c + piece)].rearrange(
-                        "p (c i t) -> p c t i", t=4, i=4
-                    ),
-                    diff[:].rearrange("p t (c i) -> p c t i", i=4),
-                    ACT.Abs,
+        def last_unit(g, b):
+            bank = query_bank(starts[g], P, b, 0)
+            h, j = divmod(starts[g], HALF)
+            for c in (0, P // 2):
+                diff = ring.tile([P, 4, P // 2], F32, name="diff")
+                nc.vector.tensor_tensor(
+                    diff[:], neg_b[h][b][:, :, j + c : j + c + P // 2],
+                    bank[:].rearrange("p (t j) -> p t j", t=4)[:, :, c : c + P // 2], ALU.add,
                 )
+                magnitude(g, b * P + c, diff)
 
         def quantize_h(g, c0=0, c1=None):
             c1 = c1 or 2 * GROUPS[g]
@@ -272,16 +284,24 @@ def tile_list_loop_closure_vetting_kernel(
         def sigmoid(logits, g, m):
             nc.scalar.activation(prob[g][:, m, :], logits, ACT.Sigmoid, bias=bv_cols[:, m : m + 1])
 
-        def verify(g, tiles):
+        def logits_of(g, tiles):
             width = GROUPS[g]
             bank = psum.tile([P, BANK], F32, name="bank")
             for n, m in enumerate(tiles):
                 for b in range(2):
                     logits_pass(bank[:, n * width : (n + 1) * width], g, m, b)
-            for n, m in enumerate(tiles):
-                sigmoid(bank[:, n * width : (n + 1) * width], g, m)
-            if 2 in tiles:
-                nc.sync.dma_start(rows_out(g), prob[g][:])
+            return [(bank[:, n * width : (n + 1) * width], m) for n, m in enumerate(tiles)]
+
+        def probabilities(g, logits, by_tile=False):
+            for sums, m in logits:
+                sigmoid(sums, g, m)
+                if by_tile:
+                    nc.sync.dma_start(rows_out(g)[:, m, :], prob[g][:, m, :])
+                elif m == 2:
+                    nc.sync.dma_start(rows_out(g), prob[g][:])
+
+        def verify(g, tiles):
+            probabilities(g, logits_of(g, tiles))
 
         def verify_last(g):
             banks = [psum.tile([P, BANK], F32, name="query_bank") for m in range(3)]
@@ -313,10 +333,10 @@ def tile_list_loop_closure_vetting_kernel(
         unit(3, 0)
         unit(3, 1)
         quantize_h(2)
-        verify(2, [0])
-        verify(2, [1, 2])
+        waiting = logits_of(2, [0]) + logits_of(2, [1, 2])
         unit(4, 0)
-        unit(4, 1)
+        last_unit(4, 1)
+        probabilities(2, waiting, by_tile=True)
         quantize_h(3)
         verify(3, [0, 1, 2])
         verify_last(4)

@@ -166,24 +166,18 @@ def tile_list_loop_closure_vetting_kernel(
         archive(0, [first0, first1], AHEAD)
         archive(1, [second0, second1], 0)
 
-        v1_first = held([P, S], U32, "v1_first")
-        gather(v1_first[:], tab[0], list1[:], U32)
-        v1_second = []
+        v1_words = [held([P, S], U32, "v1_%d" % a) for a in range(2)]
+        gather(v1_words[0][:], tab[0], list1[:], U32)
 
-        def pick_quarter(tag=None):
-            q = len(v1_second)
-            picked = held([P, QUARTER], U32, "v1_second%d" % q, tag=tag)
-            gather(picked[:], tab[1], part_of(list1, q * QUARTER, QUARTER), U32)
-            v1_second.append(picked)
+        def pick_second(j0, width):
+            gather(v1_words[1][:, j0 : j0 + width], tab[1], part_of(list1, j0, width), U32)
 
         def v1(a, j0, width):
-            if a == 0:
-                return v1_first[:, j0 : j0 + width]
-            q, j = divmod(j0, QUARTER)
-            return v1_second[q][:, j : j + width]
+            return v1_words[a][:, j0 : j0 + width]
 
-        pick_quarter()
-        pick_quarter()
+        pick_second(0, QUARTER)
+        pick_second(QUARTER, QUARTER)
+        pick_second(HALF, HALF)
 
         wv_raw = [held([P, 4 * N], F32, "wv_raw%d" % b, tag="v2_0%d" % b) for b in range(2)]
         for b in range(2):
@@ -200,12 +194,17 @@ def tile_list_loop_closure_vetting_kernel(
             return slice((2 * m + b) * P, (2 * m + b + 1) * P)
 
         def round_wv():
-            for b in range(2):
-                nc.gpsimd.tensor_scalar(
-                    wv_bf[:].rearrange("p (m b n t) -> p b m n t", b=2, n=P, t=4)[:, b],
-                    wv_raw[b][:].rearrange("p (t m n) -> p m n t", t=4, n=P),
-                    1.0, 0.0, ALU.mult, ALU.add,
+            for m in range(3):
+                cols = wv_cols(m, 0)
+                nc.scalar.copy(
+                    wv_bf[:, 4 * cols.start : 4 * cols.stop].rearrange("p (c i t) -> p c t i", t=4, i=4),
+                    wv_raw[0][:].rearrange("p (t c i) -> p c t i", t=4, i=4)[:, 32 * m : 32 * (m + 1)],
                 )
+            nc.gpsimd.tensor_scalar(
+                wv_bf[:].rearrange("p (m b n t) -> p b m n t", b=2, n=P, t=4)[:, 1],
+                wv_raw[1][:].rearrange("p (t m n) -> p m n t", t=4, n=P),
+                1.0, 0.0, ALU.mult, ALU.add,
+            )
 
         def quantize_wv(c0, c1):
             nc.vector.quantize_mx(
@@ -239,11 +238,11 @@ def tile_list_loop_closure_vetting_kernel(
                 ACT.Abs,
             )
 
-        def unit(g, b, tag=None):
+        def unit(g, b):
             width = GROUPS[g]
             slots = BANK // width
             h, j = divmod(starts[g], HALF)
-            diff = held([P, 4, width], F32, tag) if tag else ring.tile([P, 4, width], F32, name="diff")
+            diff = ring.tile([P, 4, width], F32, name="diff")
             for t0 in range(0, 4, slots):
                 bank = query_bank(starts[g], width, b, t0)
                 nc.vector.tensor_tensor(
@@ -313,19 +312,27 @@ def tile_list_loop_closure_vetting_kernel(
                 sigmoid(banks[m][:, 0:P], g, m)
                 nc.sync.dma_start(rows_out(g)[:, m, :], prob[g][:, m, :])
 
+        emptied = held([P, 4, P], F32, "emptied")
+        nc.scalar.copy(emptied[:], query_bank(0, P, 0, 0)[:].rearrange("p (t j) -> p t j", t=4))
+        aside = held([P, 4, P], F32, "aside")
+        nc.gpsimd.tensor_tensor(aside[:], emptied[:], neg_b[0][0][:, :, 0:P], ALU.add)
         round_wv()
-        unit(0, 0, tag="diff_first")
-        unit(0, 1, tag="diff_second")
-        pick_quarter("diff_first")
+        diff = ring.tile([P, 4, P], F32, name="diff")
+        nc.vector.tensor_tensor(
+            diff[:], neg_b[0][0][:, :, P : 2 * P],
+            query_bank(P, P, 0, 0)[:].rearrange("p (t j) -> p t j", t=4), ALU.add,
+        )
+        magnitude(0, P, diff)
+        unit(0, 1)
+        magnitude(0, 0, aside)
         unit(1, 0)
         unit(1, 1)
+        unit(2, 0)
         quantize_wv(0, 256)
         quantize_h(0)
         verify(0, [0])
         quantize_wv(256, 768)
         verify(0, [1, 2])
-        pick_quarter("diff_second")
-        unit(2, 0)
         unit(2, 1)
         quantize_h(1)
         verify(1, [0])

@@ -328,17 +328,21 @@ def tile_list_loop_closure_vetting_kernel(
         unit(1, 0)
         unit(1, 1)
         unit(2, 0)
+        emptied = held([P, 4, P], F32, "emptied_late")
+        nc.scalar.copy(emptied[:], query_bank(starts[3], P, 0, 0)[:].rearrange("p (t j) -> p t j", t=4))
         quantize_wv(0, 256)
         quantize_h(0)
         verify(0, [0])
         quantize_wv(256, 768)
         verify(0, [1, 2])
+        late = held([P, 4, P], F32, "aside_late", tag="wv_bf")
+        nc.gpsimd.tensor_tensor(late[:], emptied[:], neg_b[1][0][:, :, QUARTER : QUARTER + P], ALU.add)
         unit(2, 1)
+        unit(3, 1)
         quantize_h(1)
         verify(1, [0])
         verify(1, [1, 2])
-        unit(3, 0)
-        unit(3, 1)
+        magnitude(3, 0, late)
         quantize_h(2)
         waiting = logits_of(2, [0]) + logits_of(2, [1, 2])
         unit(4, 0)

@@ -252,15 +252,21 @@ def tile_list_loop_closure_vetting_kernel(
             magnitude(g, b * width, diff)
 
         def last_unit(g, b):
-            bank = query_bank(starts[g], P, b, 0)
+            half = P // 2
+            sums = query_bank(starts[g], P, b, 0)[:].rearrange("p (t j) -> p t j", t=4)
             h, j = divmod(starts[g], HALF)
-            for c in (0, P // 2):
-                diff = ring.tile([P, 4, P // 2], F32, name="diff")
-                nc.vector.tensor_tensor(
-                    diff[:], neg_b[h][b][:, :, j + c : j + c + P // 2],
-                    bank[:].rearrange("p (t j) -> p t j", t=4)[:, :, c : c + P // 2], ALU.add,
-                )
-                magnitude(g, b * P + c, diff)
+            woven = ring.tile([P, 4 * half], F32, name="diff")
+            nc.vector.tensor_tensor(
+                woven[:].rearrange("p (c i t) -> p c t i", t=4, i=4),
+                neg_b[h][b][:, :, j : j + half].rearrange("p t (c i) -> p c t i", i=4),
+                sums[:, :, 0:half].rearrange("p t (c i) -> p c t i", i=4), ALU.add,
+            )
+            diff = ring.tile([P, 4, half], F32, name="diff")
+            nc.vector.tensor_tensor(diff[:], neg_b[h][b][:, :, j + half : j + P], sums[:, :, half:P], ALU.add)
+            magnitude(g, b * P + half, diff)
+            nc.vector.scalar_tensor_tensor(
+                h_bf[g][:, 4 * b * P : 4 * (b * P + half)], woven[:], -1.0, woven[:], ALU.mult, ALU.max
+            )
 
         def quantize_h(g, c0=0, c1=None):
             c1 = c1 or 2 * GROUPS[g]

@@ -45,7 +45,7 @@ def tile_list_loop_closure_vetting_kernel(
         w8_raw = held([P, 2 * H], I32, "w8_raw")
         w8 = held([P, 2 * H], U32, "w8")
         planes = [held([P, 2 * S // 4], I32, "plane_pass0")]
-        dm_cols = held([P, 8], F32, "dm_cols")
+        dm_cols = held([P, 2, 8], F32, "dm_cols")
         warm = held([P, 1], F32, "warm")
         zero = held([P, 1], F32, "zero")
 
@@ -69,13 +69,13 @@ def tile_list_loop_closure_vetting_kernel(
             nc.sync.dma_start(words[:], tab_words[a].rearrange("p c i -> p (c i)").bitcast(I32))
             return words
 
-        nc.sync.dma_start(list2[:], offs2)
         nc.sync.dma_start(win2[ROWS, :], scale_rows(tab2_scales))
+        nc.sync.dma_start(list2[:], offs2)
         nc.sync.dma_start(w8_sc_raw[ROWS, :], scale_rows(w8_scales))
         tab2 = [load_tab2(0, "tab2_0")]
         nc.sync.dma_start(list1[:], offs)
         nc.sync.dma_start(
-            dm_cols[:].rearrange("p (b t) -> p b t", t=4), dm.rearrange("(b p t) -> p b t", b=2, t=4)
+            dm_cols[:, :, 0:4], dm.rearrange("(b p t) -> p b t", b=2, t=4)
         )
         nc.sync.dma_start(
             w8_raw[:].rearrange("p (a c) -> p a c", a=2),
@@ -149,10 +149,11 @@ def tile_list_loop_closure_vetting_kernel(
                     archive_pass(banks[r], 0, r)
                 archive_pass(banks[r], 1, r)
                 emptied = neg_b[h][r // 4][:, r % 4, :]
+                offset = dm_cols[:, r // 4, r % 4 : r % 4 + 1]
                 if 4 <= r < ahead:
-                    nc.vector.tensor_scalar(emptied, banks[r][:], -1.0, dm_cols[:, r : r + 1], ALU.mult, ALU.add)
+                    nc.vector.tensor_scalar(emptied, banks[r][:], -1.0, offset, ALU.mult, ALU.add)
                 else:
-                    nc.scalar.activation(emptied, banks[r][:], ACT.Identity, bias=dm_cols[:, r : r + 1], scale=-1.0)
+                    nc.scalar.activation(emptied, banks[r][:], ACT.Identity, bias=offset, scale=-1.0)
 
         first0, second0 = pick2(0, 0), pick2(0, 1)
         tab = [load_tab(0, "tab2_0")]

@@ -317,7 +317,8 @@ def tile_list_loop_closure_vetting_kernel(
                     logits_pass(banks[m][:, 0:P], g, m, b)
             for m in range(3):
                 sigmoid(banks[m][:, 0:P], g, m)
-                nc.sync.dma_start(rows_out(g)[:, m, :], prob[g][:, m, :])
+                queue = nc.scalar if m == 2 else nc.sync
+                queue.dma_start(rows_out(g)[:, m, :], prob[g][:, m, :])
 
         emptied = held([P, 4, P], F32, "emptied")
         nc.scalar.copy(emptied[:], query_bank(0, P, 0, 0)[:].rearrange("p (t j) -> p t j", t=4))

@@ -243,6 +243,21 @@ def tile_list_loop_closure_vetting_kernel(
             width = GROUPS[g]
             slots = BANK // width
             h, j = divmod(starts[g], HALF)
+            if slots == 2:
+                paired = ring.tile([P, 2, width, 2], F32, name="diff")
+                for u in range(2):
+                    bank = query_bank(starts[g], width, b, 2 * u)
+                    nc.vector.tensor_tensor(
+                        paired[:, u].rearrange("p (c i) e -> p c e i", i=2),
+                        neg_b[h][b][:, 2 * u : 2 * u + 2, j : j + width].rearrange("p e (c i) -> p c e i", i=2),
+                        bank[:].rearrange("p (e c i) -> p c e i", e=2, i=2), ALU.add,
+                    )
+                nc.scalar.activation(
+                    h_bf[g][:, 4 * b * width : 4 * (b + 1) * width].rearrange("p (j u e) -> p j u e", u=2, e=2),
+                    paired[:].rearrange("p u j e -> p j u e"),
+                    ACT.Abs,
+                )
+                return
             diff = ring.tile([P, 4, width], F32, name="diff")
             for t0 in range(0, 4, slots):
                 bank = query_bank(starts[g], width, b, t0)

@@ -35,7 +35,7 @@ def tile_list_loop_closure_vetting_kernel(
         psum = ctx.enter_context(tc.psum_pool(name="psum", bufs=4))
 
         def held(shape, dtype, name, tag=None):
-            return keep.tile(shape, dtype, name=name, tag=tag or name, align_bytes=64)
+            return keep.tile(shape, dtype, name=name, tag=tag or name, align_bytes=256)
 
         list1 = held([P, S // 16], U16, "list1")
         list2 = held([P, S // 16], U16, "list2")

@@ -102,7 +102,8 @@ def tile_list_loop_closure_vetting_kernel(
         def move_scales(a):
             for r in range(4):
                 first = 96 + 16 * a + r
-                nc.sync.dma_start(planes[a][r:P:32, :], stage[first : first + 13 : 4, :])
+                queue = nc.scalar if a == 0 and r < 2 else nc.sync
+                queue.dma_start(planes[a][r:P:32, :], stage[first : first + 13 : 4, :])
 
         move_scales(0)
         tab2.append(load_tab2(1, "sc2"))
@@ -195,12 +196,10 @@ def tile_list_loop_closure_vetting_kernel(
             return slice((2 * m + b) * P, (2 * m + b + 1) * P)
 
         def round_wv():
-            for m in range(3):
-                cols = wv_cols(m, 0)
-                nc.scalar.copy(
-                    wv_bf[:, 4 * cols.start : 4 * cols.stop].rearrange("p (c i t) -> p c t i", t=4, i=4),
-                    wv_raw[0][:].rearrange("p (t c i) -> p c t i", t=4, i=4)[:, 32 * m : 32 * (m + 1)],
-                )
+            nc.scalar.copy(
+                wv_bf[:].rearrange("p (m b c i t) -> p b m c t i", m=3, b=2, t=4, i=4)[:, 0],
+                wv_raw[0][:].rearrange("p (t m c i) -> p m c t i", t=4, m=3, i=4),
+            )
             nc.gpsimd.tensor_scalar(
                 wv_bf[:].rearrange("p (m b n t) -> p b m n t", b=2, n=P, t=4)[:, 1],
                 wv_raw[1][:].rearrange("p (t m n) -> p m n t", t=4, n=P),
@@ -244,7 +243,7 @@ def tile_list_loop_closure_vetting_kernel(
             slots = BANK // width
             h, j = divmod(starts[g], HALF)
             if slots == 2:
-                paired = ring.tile([P, 2, width, 2], F32, name="diff")
+                paired = ring.tile([P, 2, width, 2], F32, name="diff", align_bytes=256)
                 for u in range(2):
                     bank = query_bank(starts[g], width, b, 2 * u)
                     nc.vector.tensor_tensor(
@@ -258,7 +257,7 @@ def tile_list_loop_closure_vetting_kernel(
                     ACT.Abs,
                 )
                 return
-            diff = ring.tile([P, 4, width], F32, name="diff")
+            diff = ring.tile([P, 4, width], F32, name="diff", align_bytes=256)
             for t0 in range(0, 4, slots):
                 bank = query_bank(starts[g], width, b, t0)
                 nc.vector.tensor_tensor(
@@ -271,13 +270,13 @@ def tile_list_loop_closure_vetting_kernel(
             half = P // 2
             sums = query_bank(starts[g], P, b, 0)[:].rearrange("p (t j) -> p t j", t=4)
             h, j = divmod(starts[g], HALF)
-            woven = ring.tile([P, 4 * half], F32, name="diff")
+            woven = ring.tile([P, 4 * half], F32, name="diff", align_bytes=256)
             nc.vector.tensor_tensor(
                 woven[:].rearrange("p (c i t) -> p c t i", t=4, i=4),
                 neg_b[h][b][:, :, j : j + half].rearrange("p t (c i) -> p c t i", i=4),
                 sums[:, :, 0:half].rearrange("p t (c i) -> p c t i", i=4), ALU.add,
             )
-            diff = ring.tile([P, 4, half], F32, name="diff")
+            diff = ring.tile([P, 4, half], F32, name="diff", align_bytes=256)
             nc.vector.tensor_tensor(diff[:], neg_b[h][b][:, :, j + half : j + P], sums[:, :, half:P], ALU.add)
             magnitude(g, b * P + half, diff)
             nc.vector.scalar_tensor_tensor(
@@ -335,19 +334,17 @@ def tile_list_loop_closure_vetting_kernel(
                 queue = nc.scalar if m == 2 else nc.sync
                 queue.dma_start(rows_out(g)[:, m, :], prob[g][:, m, :])
 
-        emptied = held([P, 4, P], F32, "emptied")
-        nc.scalar.copy(emptied[:], query_bank(0, P, 0, 0)[:].rearrange("p (t j) -> p t j", t=4))
-        aside = held([P, 4, P], F32, "aside")
-        nc.gpsimd.tensor_tensor(aside[:], emptied[:], neg_b[0][0][:, :, 0:P], ALU.add)
+        emptied = held([P, 2, QUARTER], F32, "emptied")
+        nc.scalar.copy(emptied[:], query_bank(0, QUARTER, 0, 0)[:].rearrange("p (t j) -> p t j", t=2))
+        shared = held([P, 4, QUARTER], F32, "shared")
+        nc.gpsimd.tensor_tensor(shared[:, 0:2, :], emptied[:], neg_b[0][0][:, 0:2, 0:QUARTER], ALU.add)
         round_wv()
-        diff = ring.tile([P, 4, P], F32, name="diff")
         nc.vector.tensor_tensor(
-            diff[:], neg_b[0][0][:, :, P : 2 * P],
-            query_bank(P, P, 0, 0)[:].rearrange("p (t j) -> p t j", t=4), ALU.add,
+            shared[:, 2:4, :], neg_b[0][0][:, 2:4, 0:QUARTER],
+            query_bank(0, QUARTER, 0, 2)[:].rearrange("p (t j) -> p t j", t=2), ALU.add,
         )
-        magnitude(0, P, diff)
+        magnitude(0, 0, shared)
         unit(0, 1)
-        magnitude(0, 0, aside)
         unit(1, 0)
         unit(1, 1)
         unit(2, 0)

@@ -234,7 +234,7 @@ def tile_list_loop_closure_vetting_kernel(
         def magnitude(g, first, diff):
             nc.scalar.activation(
                 h_bf[g][:, 4 * first : 4 * (first + diff.shape[2])].rearrange("p (c i t) -> p c t i", t=4, i=4),
-                diff[:].rearrange("p t (c i) -> p c t i", i=4),
+                diff.rearrange("p t (c i) -> p c t i", i=4),
                 ACT.Abs,
             )
 
@@ -264,7 +264,7 @@ def tile_list_loop_closure_vetting_kernel(
                     diff[:, t0 : t0 + slots, :], neg_b[h][b][:, t0 : t0 + slots, j : j + width],
                     bank[:].rearrange("p (t j) -> p t j", t=slots), ALU.add,
                 )
-            magnitude(g, b * width, diff)
+            magnitude(g, b * width, diff[:])
 
         def last_unit(g, b):
             half = P // 2
@@ -278,7 +278,7 @@ def tile_list_loop_closure_vetting_kernel(
             )
             diff = ring.tile([P, 4, half], F32, name="diff", align_bytes=256)
             nc.vector.tensor_tensor(diff[:], neg_b[h][b][:, :, j + half : j + P], sums[:, :, half:P], ALU.add)
-            magnitude(g, b * P + half, diff)
+            magnitude(g, b * P + half, diff[:])
             nc.vector.scalar_tensor_tensor(
                 h_bf[g][:, 4 * b * P : 4 * (b * P + half)], woven[:], -1.0, woven[:], ALU.mult, ALU.max
             )
@@ -343,29 +343,33 @@ def tile_list_loop_closure_vetting_kernel(
             shared[:, 2:4, :], neg_b[0][0][:, 2:4, 0:QUARTER],
             query_bank(0, QUARTER, 0, 2)[:].rearrange("p (t j) -> p t j", t=2), ALU.add,
         )
-        magnitude(0, 0, shared)
+        magnitude(0, 0, shared[:])
         unit(0, 1)
         unit(1, 0)
         unit(1, 1)
         unit(2, 0)
-        emptied = held([P, 4, P], F32, "emptied_late")
-        nc.scalar.copy(emptied[:], query_bank(starts[3], P, 0, 0)[:].rearrange("p (t j) -> p t j", t=4))
+        emptied = held([P, 2, QUARTER], F32, "emptied_late")
+        nc.scalar.copy(emptied[:], query_bank(starts[3], QUARTER, 0, 0)[:].rearrange("p (t j) -> p t j", t=2))
         quantize_wv(0, 256)
         quantize_h(0)
         verify(0, [0])
         quantize_wv(256, 768)
         verify(0, [1, 2])
-        late = held([P, 4, P], F32, "aside_late", tag="wv_bf")
-        nc.gpsimd.tensor_tensor(late[:], emptied[:], neg_b[1][0][:, :, QUARTER : QUARTER + P], ALU.add)
+        late = held([P, 4, QUARTER], F32, "aside_late", tag="wv_bf")
+        nc.gpsimd.tensor_tensor(late[:, 0:2, :], emptied[:], neg_b[1][0][:, 0:2, QUARTER:HALF], ALU.add)
         unit(2, 1)
         unit(3, 1)
         quantize_h(1)
         verify(1, [0])
         verify(1, [1, 2])
-        magnitude(3, 0, late)
+        nc.vector.tensor_tensor(
+            late[:, 2:4, :], neg_b[1][0][:, 2:4, QUARTER:HALF],
+            query_bank(starts[3], QUARTER, 0, 2)[:].rearrange("p (t j) -> p t j", t=2), ALU.add,
+        )
+        magnitude(3, 0, late[:, :, 0:P])
         quantize_h(2)
         waiting = logits_of(2, [0]) + logits_of(2, [1, 2])
-        unit(4, 0)
+        magnitude(4, 0, late[:, :, P : 2 * P])
         last_unit(4, 1)
         probabilities(2, waiting, by_tile=True)
         quantize_h(3)

from contextlib import ExitStack

import concourse.mybir as mybir

K, T, S, H, N = 1024, 4096, 1024, 1024, 384
FLOPS = 2 * 2 * K * H * S + 2 * H * N * S

F32 = mybir.dt.float32
BF16 = mybir.dt.bfloat16
I32 = mybir.dt.int32
U32 = mybir.dt.uint32
U16 = mybir.dt.uint16
U8 = mybir.dt.uint8
FP8X4 = mybir.dt.float8_e4m3fn_x4
FP4X4 = mybir.dt.float4_e2m1fn_x4
ACT = mybir.ActivationFunctionType
ALU = mybir.AluOpType

P = 128
HALF = 512
BANK = 512
QUARTER = 256
ROWS = slice(96, 128)
GROUPS = (256, 256, 256, 128, 128)
AHEAD = 8


def tile_list_loop_closure_vetting_kernel(
    tc, tab_words, tab_scales, offs, tab2_words, tab2_scales, offs2, w8_words, w8_scales, dm, wv, bv, out
):
    nc = tc.nc
    with ExitStack() as ctx:
        keep = ctx.enter_context(tc.tile_pool(name="keep", bufs=1))
        ring = ctx.enter_context(tc.tile_pool(name="ring", bufs=6))
        psum = ctx.enter_context(tc.psum_pool(name="psum", bufs=4))

        def held(shape, dtype, name, tag=None):
            return keep.tile(shape, dtype, name=name, tag=tag or name, align_bytes=256)

        list1 = held([P, S // 16], U16, "list1")
        list2 = held([P, S // 16], U16, "list2")
        win2 = held([P, T // 4], I32, "win2")
        win1 = held([P, T // 4], I32, "win1")
        w8_sc_raw = held([P, H // 4], I32, "w8_sc_raw")
        w8_raw = held([P, 2 * H], I32, "w8_raw")
        w8 = held([P, 2 * H], U32, "w8")
        planes = [held([P, 2 * S // 4], I32, "plane_pass0")]
        dm_cols = held([P, 2, 8], F32, "dm_cols")
        warm = held([P, 1], F32, "warm")
        zero = held([P, 1], F32, "zero")

        def scale_rows(scales):
            return scales.rearrange("a q c -> (a q) c").bitcast(I32)

        nc.gpsimd.memset(w8_sc_raw[0:96, :], 0)
        nc.gpsimd.memset(planes[0][:], 0)
        nc.vector.memset(zero[:], 0.0)
        nc.vector.memset(win2[0:96, :], 0)
        nc.vector.memset(win1[:], 0)
        nc.scalar.activation(warm[:], zero[:], ACT.Sigmoid)

        def load_tab2(a, tag):
            words = held([P, T // 2], I32, "tab2_%d" % a, tag=tag)
            nc.sync.dma_start(words[:], tab2_words[a].bitcast(I32))
            return words

        def load_tab(a, tag):
            words = held([P, T], I32, "tab%d" % a, tag=tag)
            nc.sync.dma_start(words[:], tab_words[a].rearrange("p c i -> p (c i)").bitcast(I32))
            return words

        nc.sync.dma_start(win2[ROWS, :], scale_rows(tab2_scales))
        nc.sync.dma_start(list2[:], offs2)
        nc.sync.dma_start(w8_sc_raw[ROWS, :], scale_rows(w8_scales))
        tab2 = [load_tab2(0, "tab2_0")]
        nc.sync.dma_start(list1[:], offs)
        nc.sync.dma_start(
            dm_cols[:, :, 0:4], dm.rearrange("(b p t) -> p b t", b=2, t=4)
        )
        nc.sync.dma_start(
            w8_raw[:].rearrange("p (a c) -> p a c", a=2),
            w8_words.rearrange("a p c i -> p a (c i)").bitcast(I32),
        )
        nc.sync.dma_start(win1[32:96:2, :], tab_scales.rearrange("a q c -> q a c").bitcast(I32))

        def part_of(offsets, j0, width):
            return offsets[:, j0 // 16 : (j0 + width) // 16]

        def gather(picked, window, offsets, dtype):
            nc.vector.tensor_copy(picked, window[:].bitcast(dtype).indirect(offsets))

        sc2 = held([P, S], U8, "sc2")
        gather(sc2[:], win2, list2[:], U8)

        stage = held([P, 2 * S // 4], I32, "stage")
        nc.gpsimd.tensor_copy(
            stage[:].bitcast(U8)[:, 0:H].rearrange("p (b t m) -> p b t m", b=2, t=4),
            w8_sc_raw[:].bitcast(U8).rearrange("p (b m t) -> p b t m", b=2, t=4),
        )
        nc.vector.tensor_copy(stage[ROWS, 256:512], sc2[ROWS, :].bitcast(I32))

        def move_scales(a):
            for r in range(4):
                first = 96 + 16 * a + r
                queue = nc.scalar if a == 0 and r < 2 else nc.sync
                queue.dma_start(planes[a][r:P:32, :], stage[first : first + 13 : 4, :])

        move_scales(0)
        tab2.append(load_tab2(1, "sc2"))
        planes.append(held([P, 2 * S // 4], I32, "plane_pass1", tag="win2"))
        nc.gpsimd.memset(planes[1][:], 0)
        move_scales(1)

        for a in range(2):
            for b in range(2):
                cols = slice(a * H + b * HALF, a * H + (b + 1) * HALF)
                nc.scalar.copy(
                    w8[:, cols].rearrange("p (t m) -> p m t", t=4),
                    w8_raw[:, cols].bitcast(U32).rearrange("p (m t) -> p m t", t=4),
                )

        def w8_operand(a, r):
            return (
                w8[:, a * H + r * P : a * H + (r + 1) * P].bitcast(FP8X4),
                planes[a][:].bitcast(U8)[:, r * P : (r + 1) * P],
            )

        def pick2(a, h, tag=None):
            picked = held([P, HALF], U16, "v2_%d%d" % (h, a), tag=tag)
            gather(picked[:], tab2[a], part_of(list2, h * HALF, HALF), U16)
            return picked

        neg_b = [[held([P, 4, HALF], F32, "neg_b%d%d" % (h, b)) for b in range(2)] for h in range(2)]

        def archive(h, v2, ahead):
            def archive_pass(bank, a, r):
                codes, scale = w8_operand(a, r)
                nc.tensor.matmul_mx(
                    out=bank[:], lhsT=codes, lhsT_scale=scale, rhs=v2[a][:].bitcast(FP4X4),
                    rhs_scale=planes[a][:].bitcast(U8)[:, S + h * HALF : S + (h + 1) * HALF],
                    start=(a == 0), stop=(a == 1),
                )

            banks = [psum.tile([P, BANK], F32, name="bank" if r < 4 else "query_bank") for r in range(ahead)]
            for r in range(ahead):
                archive_pass(banks[r], 0, r)
            for r in range(8):
                if r >= ahead:
                    banks.append(psum.tile([P, BANK], F32, name="bank"))
                    archive_pass(banks[r], 0, r)
                archive_pass(banks[r], 1, r)
                emptied = neg_b[h][r // 4][:, r % 4, :]
                offset = dm_cols[:, r // 4, r % 4 : r % 4 + 1]
                if 4 <= r < ahead:
                    nc.vector.tensor_scalar(emptied, banks[r][:], -1.0, offset, ALU.mult, ALU.add)
                else:
                    nc.scalar.activation(emptied, banks[r][:], ACT.Identity, bias=offset, scale=-1.0)

        first0, second0 = pick2(0, 0), pick2(0, 1)
        tab = [load_tab(0, "tab2_0")]
        sc1 = held([P, S], U8, "sc1")
        gather(sc1[:], win1, list1[:], U8)
        tab.append(load_tab(1, "win1"))
        planes1 = held([P, S // 4], I32, "planes1", tag="w8_raw")
        for r in range(4):
            nc.sync.dma_start(planes1[r:P:4, :], sc1[32 + 4 * r : 96 + 4 * r : 2, :].bitcast(I32))
        first1, second1 = pick2(1, 0), pick2(1, 1)
        archive(0, [first0, first1], AHEAD)
        archive(1, [second0, second1], 0)

        v1_words = [held([P, S], U32, "v1_%d" % a) for a in range(2)]
        gather(v1_words[0][:], tab[0], list1[:], U32)

        def pick_second(j0, width):
            gather(v1_words[1][:, j0 : j0 + width], tab[1], part_of(list1, j0, width), U32)

        def v1(a, j0, width):
            return v1_words[a][:, j0 : j0 + width]

        pick_second(0, QUARTER)
        pick_second(QUARTER, QUARTER)
        pick_second(HALF, HALF)

        wv_raw = [held([P, 4 * N], F32, "wv_raw%d" % b, tag="v2_0%d" % b) for b in range(2)]
        for b in range(2):
            nc.sync.dma_start(wv_raw[b][:], wv[512 * b : 512 * (b + 1), :].rearrange("(p t) n -> p (t n)", t=4))
        bv_cols = held([P, 3], F32, "bv_cols", tag="v2_10")
        with nc.allow_non_contiguous_dma(reason="one bias value a partition"):
            nc.sync.dma_start(bv_cols[:], bv.rearrange("(m p) -> p m", p=P))

        wv_codes = held([P, 2 * N], U32, "wv_codes")
        wv_sc = held([P, 2 * N], U8, "wv_sc")
        wv_bf = held([P, 8 * N], BF16, "wv_bf")

        def wv_cols(m, b):
            return slice((2 * m + b) * P, (2 * m + b + 1) * P)

        def round_wv():
            nc.scalar.copy(
                wv_bf[:].rearrange("p (m b c i t) -> p b m c t i", m=3, b=2, t=4, i=4)[:, 0],
                wv_raw[0][:].rearrange("p (t m c i) -> p m c t i", t=4, m=3, i=4),
            )
            nc.gpsimd.tensor_scalar(
                wv_bf[:].rearrange("p (m b n t) -> p b m n t", b=2, n=P, t=4)[:, 1],
                wv_raw[1][:].rearrange("p (t m n) -> p m n t", t=4, n=P),
                1.0, 0.0, ALU.mult, ALU.add,
            )

        def quantize_wv(c0, c1):
            nc.vector.quantize_mx(
                out=wv_codes[:, c0:c1].bitcast(FP8X4), scales=wv_sc[:, c0:c1], in_=wv_bf[:, 4 * c0 : 4 * c1]
            )

        starts = [sum(GROUPS[:g]) for g in range(len(GROUPS))]
        h_bf = [held([P, 8 * width], BF16, "h_bf%d" % g) for g, width in enumerate(GROUPS)]
        h_codes = [held([P, 2 * width], U32, "h_codes%d" % g) for g, width in enumerate(GROUPS)]
        h_sc = [held([P, 2 * width], U8, "h_sc%d" % g) for g, width in enumerate(GROUPS)]
        prob = [held([P, 3, width], F32, "prob%d" % g) for g, width in enumerate(GROUPS)]

        def query_bank(j0, width, b, t0):
            slots = BANK // width
            bank = psum.tile([P, BANK], F32, name="query_bank")
            for a in range(2):
                for t in range(slots):
                    codes, scale = w8_operand(a, 4 * b + t0 + t)
                    nc.tensor.matmul_mx(
                        out=bank[:, t * width : (t + 1) * width], lhsT=codes, lhsT_scale=scale,
                        rhs=v1(a, j0, width).bitcast(FP8X4),
                        rhs_scale=planes1[:].bitcast(U8)[4 * a : P, j0 : j0 + width],
                        start=(a == 0 and t == 0), stop=(a == 1 and t == slots - 1),
                    )
            return bank

        def magnitude(g, first, diff):
            nc.scalar.activation(
                h_bf[g][:, 4 * first : 4 * (first + diff.shape[2])].rearrange("p (c i t) -> p c t i", t=4, i=4),
                diff.rearrange("p t (c i) -> p c t i", i=4),
                ACT.Abs,
            )

        def unit(g, b):
            width = GROUPS[g]
            slots = BANK // width
            h, j = divmod(starts[g], HALF)
            if slots == 2:
                paired = ring.tile([P, 2, width, 2], F32, name="diff", align_bytes=256)
                for u in range(2):
                    bank = query_bank(starts[g], width, b, 2 * u)
                    nc.vector.tensor_tensor(
                        paired[:, u].rearrange("p (c i) e -> p c e i", i=2),
                        neg_b[h][b][:, 2 * u : 2 * u + 2, j : j + width].rearrange("p e (c i) -> p c e i", i=2),
                        bank[:].rearrange("p (e c i) -> p c e i", e=2, i=2), ALU.add,
                    )
                nc.scalar.activation(
                    h_bf[g][:, 4 * b * width : 4 * (b + 1) * width].rearrange("p (j u e) -> p j u e", u=2, e=2),
                    paired[:].rearrange("p u j e -> p j u e"),
                    ACT.Abs,
                )
                return
            diff = ring.tile([P, 4, width], F32, name="diff", align_bytes=256)
            for t0 in range(0, 4, slots):
                bank = query_bank(starts[g], width, b, t0)
                nc.vector.tensor_tensor(
                    diff[:, t0 : t0 + slots, :], neg_b[h][b][:, t0 : t0 + slots, j : j + width],
                    bank[:].rearrange("p (t j) -> p t j", t=slots), ALU.add,
                )
            magnitude(g, b * width, diff[:])

        def last_unit(g, b):
            half = P // 2
            sums = query_bank(starts[g], P, b, 0)[:].rearrange("p (t j) -> p t j", t=4)
            h, j = divmod(starts[g], HALF)
            woven = ring.tile([P, 4 * half], F32, name="diff", align_bytes=256)
            nc.vector.tensor_tensor(
                woven[:].rearrange("p (c i t) -> p c t i", t=4, i=4),
                neg_b[h][b][:, :, j : j + half].rearrange("p t (c i) -> p c t i", i=4),
                sums[:, :, 0:half].rearrange("p t (c i) -> p c t i", i=4), ALU.add,
            )
            diff = ring.tile([P, 4, half], F32, name="diff", align_bytes=256)
            nc.vector.tensor_tensor(diff[:], neg_b[h][b][:, :, j + half : j + P], sums[:, :, half:P], ALU.add)
            magnitude(g, b * P + half, diff[:])
            nc.vector.scalar_tensor_tensor(
                h_bf[g][:, 4 * b * P : 4 * (b * P + half)], woven[:], -1.0, woven[:], ALU.mult, ALU.max
            )

        def quantize_h(g, c0=0, c1=None):
            c1 = c1 or 2 * GROUPS[g]
            nc.vector.quantize_mx(
                out=h_codes[g][:, c0:c1].bitcast(FP8X4), scales=h_sc[g][:, c0:c1], in_=h_bf[g][:, 4 * c0 : 4 * c1]
            )

        def logits_pass(logits, g, m, b):
            width = GROUPS[g]
            nc.tensor.matmul_mx(
                out=logits, lhsT=wv_codes[:, wv_cols(m, b)].bitcast(FP8X4), lhsT_scale=wv_sc[:, wv_cols(m, b)],
                rhs=h_codes[g][:, b * width : (b + 1) * width].bitcast(FP8X4),
                rhs_scale=h_sc[g][:, b * width : (b + 1) * width],
                start=(b == 0), stop=(b == 1),
            )

        def rows_out(g):
            return out.rearrange("(m p) j -> p m j", p=P)[:, :, starts[g] : starts[g] + GROUPS[g]]

        def sigmoid(logits, g, m):
            nc.scalar.activation(prob[g][:, m, :], logits, ACT.Sigmoid, bias=bv_cols[:, m : m + 1])

        def logits_of(g, tiles):
            width = GROUPS[g]
            bank = psum.tile([P, BANK], F32, name="bank")
            for n, m in enumerate(tiles):
                for b in range(2):
                    logits_pass(bank[:, n * width : (n + 1) * width], g, m, b)
            return [(bank[:, n * width : (n + 1) * width], m) for n, m in enumerate(tiles)]

        def probabilities(g, logits, by_tile=False):
            for sums, m in logits:
                sigmoid(sums, g, m)
                if by_tile:
                    nc.sync.dma_start(rows_out(g)[:, m, :], prob[g][:, m, :])
                elif m == 2:
                    nc.sync.dma_start(rows_out(g), prob[g][:])

        def verify(g, tiles):
            probabilities(g, logits_of(g, tiles))

        def verify_last(g):
            banks = [psum.tile([P, BANK], F32, name="query_bank") for m in range(3)]
            for b in range(2):
                quantize_h(g, b * P, (b + 1) * P)
                for m in range(3):
                    logits_pass(banks[m][:, 0:P], g, m, b)
            for m in range(3):
                sigmoid(banks[m][:, 0:P], g, m)
                queue = nc.scalar if m == 2 else nc.sync
                queue.dma_start(rows_out(g)[:, m, :], prob[g][:, m, :])

        emptied = held([P, 2, QUARTER], F32, "emptied")
        nc.scalar.copy(emptied[:], query_bank(0, QUARTER, 0, 0)[:].rearrange("p (t j) -> p t j", t=2))
        shared = held([P, 4, QUARTER], F32, "shared")
        nc.gpsimd.tensor_tensor(shared[:, 0:2, :], emptied[:], neg_b[0][0][:, 0:2, 0:QUARTER], ALU.add)
        round_wv()
        nc.vector.tensor_tensor(
            shared[:, 2:4, :], neg_b[0][0][:, 2:4, 0:QUARTER],
            query_bank(0, QUARTER, 0, 2)[:].rearrange("p (t j) -> p t j", t=2), ALU.add,
        )
        magnitude(0, 0, shared[:])
        unit(0, 1)
        unit(1, 0)
        unit(1, 1)
        unit(2, 0)
        emptied = held([P, 2, QUARTER], F32, "emptied_late")
        nc.scalar.copy(emptied[:], query_bank(starts[3], QUARTER, 0, 0)[:].rearrange("p (t j) -> p t j", t=2))
        quantize_wv(0, 256)
        quantize_h(0)
        verify(0, [0])
        quantize_wv(256, 768)
        verify(0, [1, 2])
        late = held([P, 4, QUARTER], F32, "aside_late", tag="wv_bf")
        nc.gpsimd.tensor_tensor(late[:, 0:2, :], emptied[:], neg_b[1][0][:, 0:2, QUARTER:HALF], ALU.add)
        unit(2, 1)
        unit(3, 1)
        quantize_h(1)
        verify(1, [0])
        verify(1, [1, 2])
        nc.vector.tensor_tensor(
            late[:, 2:4, :], neg_b[1][0][:, 2:4, QUARTER:HALF],
            query_bank(starts[3], QUARTER, 0, 2)[:].rearrange("p (t j) -> p t j", t=2), ALU.add,
        )
        magnitude(3, 0, late[:, :, 0:P])
        quantize_h(2)
        waiting = logits_of(2, [0]) + logits_of(2, [1, 2])
        magnitude(4, 0, late[:, :, P : 2 * P])
        last_unit(4, 1)
        probabilities(2, waiting, by_tile=True)
        quantize_h(3)
        verify(3, [0, 1, 2])
        verify_last(4)
